import numpy as np
import ml_dtypes


def mxq(x, axis, fmt="e4m3"):
    dtype, down = {"e4m3": (ml_dtypes.float8_e4m3fn, 7), "e5m2": (ml_dtypes.float8_e5m2, 14)}[fmt]
    v = np.moveaxis(np.asarray(x, np.float32).astype(ml_dtypes.bfloat16).astype(np.float64), axis, -1)
    blocks = v.reshape(v.shape[:-1] + (-1, 32))
    amax = np.abs(blocks).max(-1, keepdims=True)
    byte = np.maximum(np.where(amax > 0, np.frexp(amax)[1] - 1 + 127, 0) - down, 1)
    scale = np.exp2(byte - 127.0)
    codes = (blocks / scale).astype(np.float32).astype(dtype).astype(np.float64)
    return np.moveaxis((codes * scale).reshape(v.shape), -1, axis)


WIDE = False


def mx_kscale(k):
    if not WIDE:
        return np.ones(k)
    levels = np.array([10, -10, 5, -5, 0])
    if k % 512:
        return np.exp2(np.random.permutation(np.resize(levels, k // 32))).repeat(32)
    a = np.empty((k // 512, 16))
    for p in range(k // 512):
        a[p, :8] = np.random.permutation(np.resize(levels, 8))
        for g in range(8):
            far = levels[np.abs(levels - a[p, g]) >= 10]
            a[p, g + 8] = far[np.random.randint(len(far))]
    return np.exp2(a.ravel()).repeat(32)


def f64(x):
    return np.asarray(x).astype(np.float64)


def striped8(idx):
    return np.asarray(idx).reshape(8, -1, 16).transpose(0, 2, 1).reshape(128, -1).astype(np.uint16)


def unstriped8(offs):
    return offs.reshape(8, 16, -1).transpose(0, 2, 1).reshape(8, -1).astype(np.int64)


def pick8(x, idx, run):
    r = np.arange(len(x))
    return x[r[:, None], idx[r % (8 * run) // run]]


D, T, Q, I, J = 512, 2048, 128, 512, 512


def setup_inputs():
    n = np.random.standard_normal
    idx = np.stack([np.random.permutation(T)[:I] for _ in range(8)])
    idx2 = np.stack([np.random.permutation(T)[:J] for _ in range(8)])
    fd = mx_kscale(D)
    return {
        "query": (n((D, Q)) * 0.6 / np.sqrt(D) * fd[:, None]).astype(np.float32),
        "keys": (n((D, T)) / fd[:, None]).astype(np.float32),
        "mass": (np.random.uniform(0.0, 2.0, (Q, T))).astype(np.float32),
        "dec": (np.random.uniform(0.8, 1.0, (Q, 1))).astype(np.float32),
        "offs": striped8(idx),
        "offs2": striped8(idx2),
    }


def reference(query, keys, mass, dec, offs, offs2):
    idx = unstriped8(offs)
    idx2 = unstriped8(offs2)
    queryq = mxq(f64(query), 0, "e4m3")
    keysq = mxq(f64(keys), 0, "e4m3")
    a = queryq.T @ keysq
    p = np.exp(pick8(a, idx, 16))
    w = p / np.sum(p, axis=1, keepdims=True) * 512.0
    wf = np.zeros((Q, T))
    wf[np.arange(Q)[:, None], idx[np.arange(Q) % 128 // 16]] = w
    x = f64(dec) * f64(mass) + wf
    y = pick8(x, idx2, 16) * 2.0
    return y

@@ -1,0 +1,112 @@
+from contextlib import ExitStack
+
+import concourse.mybir as mybir
+
+D, T, Q, I, J = 512, 2048, 128, 512, 512
+FLOPS = 2 * D * T * Q
+
+F32 = mybir.dt.float32
+BF16 = mybir.dt.bfloat16
+U32 = mybir.dt.uint32
+U16 = mybir.dt.uint16
+U8 = mybir.dt.uint8
+FP8X4 = mybir.dt.float8_e4m3fn_x4
+ALU = mybir.AluOpType
+ACT = mybir.ActivationFunctionType
+
+P = 128
+PACK = 4
+CHUNKS = ((512, 320), (512, 320), (512, 320), (256, 176), (256, 176))
+FIRST = 128
+
+
+def interleave(copy, grouped, raw, lo, hi):
+    copy(
+        out=grouped[:, lo:hi, :].rearrange("p (c i) j -> p c j i", i=4),
+        in_=raw[:, :, lo:hi].rearrange("p j (c i) -> p c j i", i=4),
+    )
+
+
+def tile_attend_evictscores_heads_kernel(tc, query, keys, mass, dec, offs, offs2, out):
+    nc = tc.nc
+    with ExitStack() as ctx:
+        keep = ctx.enter_context(tc.tile_pool(name="keep", bufs=1))
+        psum = ctx.enter_context(tc.psum_pool(name="psum", bufs=1))
+
+        q_raw = keep.tile([P, PACK, Q], F32, name="q_raw")
+        nc.sync.dma_start(out=q_raw[:], in_=query.rearrange("(p j) q -> p j q", j=PACK))
+        k_view = keys.rearrange("(p j) t -> p j t", j=PACK)
+        k_raw = []
+        t0 = 0
+        for c, (width, share) in enumerate(CHUNKS):
+            raw = keep.tile([P, PACK, width], F32, name=f"k_raw{c}")
+            nc.sync.dma_start(out=raw[:], in_=k_view[:, :, t0 : t0 + width])
+            k_raw.append(raw)
+            t0 = t0 + width
+        slots = keep.tile([P, I // 16], U16, name="slots")
+        nc.sync.dma_start(slots[:], offs)
+        mass_sb = keep.tile([P, T], F32, name="mass_sb")
+        nc.sync.dma_start(out=mass_sb[:], in_=mass)
+        dec_sb = keep.tile([P, 1], F32, name="dec_sb")
+        nc.sync.dma_start(out=dec_sb[:], in_=dec)
+        cands = keep.tile([P, J // 16], U16, name="cands")
+        nc.sync.dma_start(cands[:], offs2)
+
+
+        placed = keep.tile([P, T], F32, name="placed")
+        nc.vector.memset(placed[:], 0.0)
+        gain = keep.tile([P, I], F32, name="gain")
+        nc.gpsimd.memset(gain[:], 512.0)
+
+        q_bf = keep.tile([P, Q, PACK], BF16, name="q_bf", align_bytes=64)
+        interleave(nc.vector.tensor_copy, q_bf, q_raw, 0, Q)
+        q_codes = keep.tile([P, Q], U32, name="q_codes", align_bytes=64)
+        q_scales = keep.tile([P, Q], U8, name="q_scales", align_bytes=64)
+        nc.vector.quantize_mx(out=q_codes[:].bitcast(FP8X4), scales=q_scales[:], in_=q_bf[:].rearrange("p w j -> p (w j)"))
+
+        scores = keep.tile([P, T], F32, name="scores")
+        t0 = 0
+        for c, (width, share) in enumerate(CHUNKS):
+            k_bf = keep.tile([P, width, PACK], BF16, name=f"k_bf{c}", align_bytes=64)
+            interleave(nc.vector.tensor_copy, k_bf, k_raw[c], 0, share)
+            interleave(nc.scalar.copy, k_bf, k_raw[c], share, width)
+            k_codes = keep.tile([P, width], U32, name=f"k_codes{c}", align_bytes=64)
+            k_scales = keep.tile([P, width], U8, name=f"k_scales{c}", align_bytes=64)
+            nc.vector.quantize_mx(out=k_codes[:].bitcast(FP8X4), scales=k_scales[:], in_=k_bf[:].rearrange("p w j -> p (w j)"))
+            acc = psum.tile([Q, width], F32, name=f"acc{c}")
+            nc.tensor.matmul_mx(
+                out=acc[:],
+                lhsT=q_codes[:].bitcast(FP8X4),
+                lhsT_scale=q_scales[:],
+                rhs=k_codes[:].bitcast(FP8X4),
+                rhs_scale=k_scales[:],
+                start=True,
+                stop=True,
+            )
+            nc.scalar.copy(out=scores[:, t0 : t0 + width], in_=acc[:])
+            t0 = t0 + width
+
+        listed = keep.tile([P, I], F32, name="listed", tag="listed_decayed")
+        nc.vector.tensor_copy(listed[:], scores[:].indirect(slots[:]))
+        neg_max = keep.tile([P, 1], F32, name="neg_max")
+        nc.vector.tensor_reduce(out=neg_max[:], in_=listed[:], axis=mybir.AxisListType.X, op=ALU.max, negate=True)
+        p_first = keep.tile([P, FIRST], F32, name="p_first")
+        nc.scalar.activation(out=p_first[:], in_=listed[:, :FIRST], func=ACT.Exp, bias=neg_max[:])
+        p_all = keep.tile([P, I], F32, name="p_all")
+        p_sum = keep.tile([P, 1], F32, name="p_sum")
+        nc.scalar.activation(out=p_all[:], in_=listed[:], func=ACT.Exp, bias=neg_max[:], accum_out=p_sum[:])
+
+        nc.vector.tensor_tensor(placed[:].indirect(slots[:, : FIRST // 16]), p_first[:], gain[:, :FIRST], ALU.mult)
+        inv_sum = keep.tile([P, 1], F32, name="inv_sum")
+        nc.vector.reciprocal(out=inv_sum[:], in_=p_sum[:])
+        nc.vector.tensor_tensor(placed[:].indirect(slots[:, FIRST // 16 :]), p_all[:, FIRST:], gain[:, FIRST:], ALU.mult)
+
+        decayed = keep.tile([P, T], F32, name="decayed", tag="listed_decayed")
+        nc.scalar.activation(out=decayed[:], in_=mass_sb[:], func=ACT.Copy, scale=dec_sb[:])
+        updated = keep.tile([P, T], F32, name="updated")
+        nc.vector.scalar_tensor_tensor(
+            out=updated[:], in0=placed[:], scalar=inv_sum[:], in1=decayed[:], op0=ALU.mult, op1=ALU.add
+        )
+        result = keep.tile([P, J], F32, name="result")
+        nc.vector.tensor_scalar(result[:], updated[:].indirect(cands[:]), 2.0, 0.0, ALU.mult, ALU.add)
+        nc.sync.dma_start(out=out, in_=result[:])

@@ -16,8 +16,9 @@ ACT = mybir.ActivationFunctionType
 
 P = 128
 PACK = 4
-CHUNKS = ((512, 320), (512, 320), (512, 320), (256, 176), (256, 176))
+CHUNKS = ((512, 288, 512), (512, 288, 512), (256, 168, 256), (256, 256, 256), (256, 256, 256), (256, 256, 128))
 FIRST = 128
+QUERY_AT = 3
 
 
 def interleave(copy, grouped, raw, lo, hi):
@@ -34,11 +35,12 @@ def tile_attend_evictscores_heads_kernel(tc, query, keys, mass, dec, offs, offs2
         psum = ctx.enter_context(tc.psum_pool(name="psum", bufs=1))
 
         q_raw = keep.tile([P, PACK, Q], F32, name="q_raw")
-        nc.sync.dma_start(out=q_raw[:], in_=query.rearrange("(p j) q -> p j q", j=PACK))
         k_view = keys.rearrange("(p j) t -> p j t", j=PACK)
         k_raw = []
         t0 = 0
-        for c, (width, share) in enumerate(CHUNKS):
+        for c, (width, share, n_tile) in enumerate(CHUNKS):
+            if c == QUERY_AT:
+                nc.sync.dma_start(out=q_raw[:], in_=query.rearrange("(p j) q -> p j q", j=PACK))
             raw = keep.tile([P, PACK, width], F32, name=f"k_raw{c}")
             nc.sync.dma_start(out=raw[:], in_=k_view[:, :, t0 : t0 + width])
             k_raw.append(raw)
@@ -52,6 +54,10 @@ def tile_attend_evictscores_heads_kernel(tc, query, keys, mass, dec, offs, offs2
         cands = keep.tile([P, J // 16], U16, name="cands")
         nc.sync.dma_start(cands[:], offs2)
 
+        warm = keep.tile([P, 1], F32, name="warm")
+        nc.vector.memset(warm[:], 0.0)
+        warm_out = keep.tile([P, 1], F32, name="warm_out")
+        nc.scalar.activation(out=warm_out[:], in_=warm[:], func=ACT.Exp)
 
         placed = keep.tile([P, T], F32, name="placed")
         nc.vector.memset(placed[:], 0.0)
@@ -59,31 +65,40 @@ def tile_attend_evictscores_heads_kernel(tc, query, keys, mass, dec, offs, offs2
         nc.gpsimd.memset(gain[:], 512.0)
 
         q_bf = keep.tile([P, Q, PACK], BF16, name="q_bf", align_bytes=64)
-        interleave(nc.vector.tensor_copy, q_bf, q_raw, 0, Q)
+        interleave(nc.scalar.copy, q_bf, q_raw, 0, Q)
         q_codes = keep.tile([P, Q], U32, name="q_codes", align_bytes=64)
         q_scales = keep.tile([P, Q], U8, name="q_scales", align_bytes=64)
         nc.vector.quantize_mx(out=q_codes[:].bitcast(FP8X4), scales=q_scales[:], in_=q_bf[:].rearrange("p w j -> p (w j)"))
 
         scores = keep.tile([P, T], F32, name="scores")
         t0 = 0
-        for c, (width, share) in enumerate(CHUNKS):
+        for c, (width, share, n_tile) in enumerate(CHUNKS):
+            half = width // 2
             k_bf = keep.tile([P, width, PACK], BF16, name=f"k_bf{c}", align_bytes=64)
-            interleave(nc.vector.tensor_copy, k_bf, k_raw[c], 0, share)
-            interleave(nc.scalar.copy, k_bf, k_raw[c], share, width)
             k_codes = keep.tile([P, width], U32, name=f"k_codes{c}", align_bytes=64)
             k_scales = keep.tile([P, width], U8, name=f"k_scales{c}", align_bytes=64)
-            nc.vector.quantize_mx(out=k_codes[:].bitcast(FP8X4), scales=k_scales[:], in_=k_bf[:].rearrange("p w j -> p (w j)"))
-            acc = psum.tile([Q, width], F32, name=f"acc{c}")
-            nc.tensor.matmul_mx(
-                out=acc[:],
-                lhsT=q_codes[:].bitcast(FP8X4),
-                lhsT_scale=q_scales[:],
-                rhs=k_codes[:].bitcast(FP8X4),
-                rhs_scale=k_scales[:],
-                start=True,
-                stop=True,
-            )
-            nc.scalar.copy(out=scores[:, t0 : t0 + width], in_=acc[:])
+            interleave(nc.vector.tensor_copy, k_bf, k_raw[c], 0, half)
+            interleave(nc.vector.tensor_copy, k_bf, k_raw[c], half, share)
+            if share < width:
+                interleave(nc.scalar.copy, k_bf, k_raw[c], share, width)
+            for lo in (0, half):
+                nc.vector.quantize_mx(
+                    out=k_codes[:, lo : lo + half].bitcast(FP8X4),
+                    scales=k_scales[:, lo : lo + half],
+                    in_=k_bf[:, lo : lo + half, :].rearrange("p w j -> p (w j)"),
+                )
+            for lo in range(0, width, n_tile):
+                acc = psum.tile([Q, n_tile], F32, name=f"acc{c}_{lo}")
+                nc.tensor.matmul_mx(
+                    out=acc[:],
+                    lhsT=q_codes[:].bitcast(FP8X4),
+                    lhsT_scale=q_scales[:],
+                    rhs=k_codes[:, lo : lo + n_tile].bitcast(FP8X4),
+                    rhs_scale=k_scales[:, lo : lo + n_tile],
+                    start=True,
+                    stop=True,
+                )
+                nc.scalar.copy(out=scores[:, t0 + lo : t0 + lo + n_tile], in_=acc[:])
             t0 = t0 + width
 
         listed = keep.tile([P, I], F32, name="listed", tag="listed_decayed")

@@ -16,9 +16,9 @@ ACT = mybir.ActivationFunctionType
 
 P = 128
 PACK = 4
-CHUNKS = ((512, 288, 512), (512, 288, 512), (256, 168, 256), (256, 256, 256), (256, 256, 256), (256, 256, 128))
+CHUNKS = ((1024, 576, 256, 512), (512, 256, 256, 512), (256, 256, 128, 256), (256, 256, 128, 128))
 FIRST = 128
-QUERY_AT = 3
+QUERY_AT = 2
 
 
 def interleave(copy, grouped, raw, lo, hi):
@@ -38,7 +38,7 @@ def tile_attend_evictscores_heads_kernel(tc, query, keys, mass, dec, offs, offs2
         k_view = keys.rearrange("(p j) t -> p j t", j=PACK)
         k_raw = []
         t0 = 0
-        for c, (width, share, n_tile) in enumerate(CHUNKS):
+        for c, (width, share, step, n_tile) in enumerate(CHUNKS):
             if c == QUERY_AT:
                 nc.sync.dma_start(out=q_raw[:], in_=query.rearrange("(p j) q -> p j q", j=PACK))
             raw = keep.tile([P, PACK, width], F32, name=f"k_raw{c}")
@@ -65,27 +65,28 @@ def tile_attend_evictscores_heads_kernel(tc, query, keys, mass, dec, offs, offs2
         nc.gpsimd.memset(gain[:], 512.0)
 
         q_bf = keep.tile([P, Q, PACK], BF16, name="q_bf", align_bytes=64)
-        interleave(nc.scalar.copy, q_bf, q_raw, 0, Q)
+        interleave(nc.vector.tensor_copy, q_bf, q_raw, 0, Q)
         q_codes = keep.tile([P, Q], U32, name="q_codes", align_bytes=64)
         q_scales = keep.tile([P, Q], U8, name="q_scales", align_bytes=64)
         nc.vector.quantize_mx(out=q_codes[:].bitcast(FP8X4), scales=q_scales[:], in_=q_bf[:].rearrange("p w j -> p (w j)"))
 
         scores = keep.tile([P, T], F32, name="scores")
         t0 = 0
-        for c, (width, share, n_tile) in enumerate(CHUNKS):
-            half = width // 2
+        for c, (width, share, step, n_tile) in enumerate(CHUNKS):
             k_bf = keep.tile([P, width, PACK], BF16, name=f"k_bf{c}", align_bytes=64)
             k_codes = keep.tile([P, width], U32, name=f"k_codes{c}", align_bytes=64)
             k_scales = keep.tile([P, width], U8, name=f"k_scales{c}", align_bytes=64)
-            interleave(nc.vector.tensor_copy, k_bf, k_raw[c], 0, half)
-            interleave(nc.vector.tensor_copy, k_bf, k_raw[c], half, share)
-            if share < width:
-                interleave(nc.scalar.copy, k_bf, k_raw[c], share, width)
-            for lo in (0, half):
+            for lo in range(0, width, step):
+                hi = lo + step
+                if lo < share:
+                    interleave(nc.vector.tensor_copy, k_bf, k_raw[c], lo, min(hi, share))
+                if hi > share:
+                    interleave(nc.scalar.copy, k_bf, k_raw[c], max(lo, share), hi)
+            for lo in range(0, width, step):
                 nc.vector.quantize_mx(
-                    out=k_codes[:, lo : lo + half].bitcast(FP8X4),
-                    scales=k_scales[:, lo : lo + half],
-                    in_=k_bf[:, lo : lo + half, :].rearrange("p w j -> p (w j)"),
+                    out=k_codes[:, lo : lo + step].bitcast(FP8X4),
+                    scales=k_scales[:, lo : lo + step],
+                    in_=k_bf[:, lo : lo + step, :].rearrange("p w j -> p (w j)"),
                 )
             for lo in range(0, width, n_tile):
                 acc = psum.tile([Q, n_tile], F32, name=f"acc{c}_{lo}")
@@ -98,7 +99,8 @@ def tile_attend_evictscores_heads_kernel(tc, query, keys, mass, dec, offs, offs2
                     start=True,
                     stop=True,
                 )
-                nc.scalar.copy(out=scores[:, t0 + lo : t0 + lo + n_tile], in_=acc[:])
+                leave = nc.vector.tensor_copy if c == len(CHUNKS) - 1 else nc.scalar.copy
+                leave(out=scores[:, t0 + lo : t0 + lo + n_tile], in_=acc[:])
             t0 = t0 + width
 
         listed = keep.tile([P, I], F32, name="listed", tag="listed_decayed")

@@ -54,10 +54,6 @@ def tile_attend_evictscores_heads_kernel(tc, query, keys, mass, dec, offs, offs2
         cands = keep.tile([P, J // 16], U16, name="cands")
         nc.sync.dma_start(cands[:], offs2)
 
-        warm = keep.tile([P, 1], F32, name="warm")
-        nc.vector.memset(warm[:], 0.0)
-        warm_out = keep.tile([P, 1], F32, name="warm_out")
-        nc.scalar.activation(out=warm_out[:], in_=warm[:], func=ACT.Exp)
 
         placed = keep.tile([P, T], F32, name="placed")
         nc.vector.memset(placed[:], 0.0)

@@ -47,18 +47,18 @@ def tile_attend_evictscores_heads_kernel(tc, query, keys, mass, dec, offs, offs2
             t0 = t0 + width
         slots = keep.tile([P, I // 16], U16, name="slots")
         nc.sync.dma_start(slots[:], offs)
-        mass_sb = keep.tile([P, T], F32, name="mass_sb")
-        nc.sync.dma_start(out=mass_sb[:], in_=mass)
         dec_sb = keep.tile([P, 1], F32, name="dec_sb")
         nc.sync.dma_start(out=dec_sb[:], in_=dec)
+        mass_lo = keep.tile([P, T // 2], F32, name="mass_lo", tag="mass_lo_p_first")
+        nc.sync.dma_start(out=mass_lo[:], in_=mass[:, : T // 2])
+        mass_hi = keep.tile([P, T // 2], F32, name="mass_hi")
+        nc.sync.dma_start(out=mass_hi[:], in_=mass[:, T // 2 :])
         cands = keep.tile([P, J // 16], U16, name="cands")
         nc.sync.dma_start(cands[:], offs2)
 
 
         placed = keep.tile([P, T], F32, name="placed")
         nc.vector.memset(placed[:], 0.0)
-        gain = keep.tile([P, I], F32, name="gain")
-        nc.gpsimd.memset(gain[:], 512.0)
 
         q_bf = keep.tile([P, Q, PACK], BF16, name="q_bf", align_bytes=64)
         interleave(nc.vector.tensor_copy, q_bf, q_raw, 0, Q)
@@ -99,27 +99,34 @@ def tile_attend_evictscores_heads_kernel(tc, query, keys, mass, dec, offs, offs2
                 leave(out=scores[:, t0 + lo : t0 + lo + n_tile], in_=acc[:])
             t0 = t0 + width
 
+        decayed_lo = keep.tile([P, T // 2], F32, name="decayed_lo")
+        nc.scalar.activation(out=decayed_lo[:], in_=mass_lo[:], func=ACT.Copy, scale=dec_sb[:])
         listed = keep.tile([P, I], F32, name="listed", tag="listed_decayed")
         nc.vector.tensor_copy(listed[:], scores[:].indirect(slots[:]))
         neg_max = keep.tile([P, 1], F32, name="neg_max")
         nc.vector.tensor_reduce(out=neg_max[:], in_=listed[:], axis=mybir.AxisListType.X, op=ALU.max, negate=True)
-        p_first = keep.tile([P, FIRST], F32, name="p_first")
-        nc.scalar.activation(out=p_first[:], in_=listed[:, :FIRST], func=ACT.Exp, bias=neg_max[:])
-        p_all = keep.tile([P, I], F32, name="p_all")
+        p_both = keep.tile([P, FIRST + I], F32, name="p_both", tag="mass_lo_p_first")
+        p_first = p_both[:, :FIRST]
+        p_all = p_both[:, FIRST:]
+        nc.scalar.activation(out=p_first, in_=listed[:, :FIRST], func=ACT.Exp, bias=neg_max[:])
         p_sum = keep.tile([P, 1], F32, name="p_sum")
-        nc.scalar.activation(out=p_all[:], in_=listed[:], func=ACT.Exp, bias=neg_max[:], accum_out=p_sum[:])
+        nc.scalar.activation(out=p_all, in_=listed[:], func=ACT.Exp, bias=neg_max[:], accum_out=p_sum[:])
 
-        nc.vector.tensor_tensor(placed[:].indirect(slots[:, : FIRST // 16]), p_first[:], gain[:, :FIRST], ALU.mult)
+        nc.vector.tensor_copy(placed[:].indirect(slots[:, : FIRST // 16]), p_first)
         inv_sum = keep.tile([P, 1], F32, name="inv_sum")
         nc.vector.reciprocal(out=inv_sum[:], in_=p_sum[:])
-        nc.vector.tensor_tensor(placed[:].indirect(slots[:, FIRST // 16 :]), p_all[:, FIRST:], gain[:, FIRST:], ALU.mult)
+        nc.vector.tensor_copy(placed[:].indirect(slots[:, FIRST // 16 :]), p_both[:, 2 * FIRST :])
 
-        decayed = keep.tile([P, T], F32, name="decayed", tag="listed_decayed")
-        nc.scalar.activation(out=decayed[:], in_=mass_sb[:], func=ACT.Copy, scale=dec_sb[:])
+        decayed_hi = keep.tile([P, T // 2], F32, name="decayed_hi", tag="listed_decayed")
+        nc.scalar.activation(out=decayed_hi[:], in_=mass_hi[:], func=ACT.Copy, scale=dec_sb[:])
+        gain = keep.tile([P, 1], F32, name="gain")
+        nc.scalar.activation(out=gain[:], in_=inv_sum[:], func=ACT.Copy, scale=512.0)
         updated = keep.tile([P, T], F32, name="updated")
-        nc.vector.scalar_tensor_tensor(
-            out=updated[:], in0=placed[:], scalar=inv_sum[:], in1=decayed[:], op0=ALU.mult, op1=ALU.add
-        )
+        for half, decayed in enumerate((decayed_lo, decayed_hi)):
+            cols = slice(half * T // 2, (half + 1) * T // 2)
+            nc.vector.scalar_tensor_tensor(
+                out=updated[:, cols], in0=placed[:, cols], scalar=gain[:], in1=decayed[:], op0=ALU.mult, op1=ALU.add
+            )
         result = keep.tile([P, J], F32, name="result")
         nc.vector.tensor_scalar(result[:], updated[:].indirect(cands[:]), 2.0, 0.0, ALU.mult, ALU.add)
         nc.sync.dma_start(out=out, in_=result[:])

@@ -1,6 +1,7 @@
 from contextlib import ExitStack
 
 import concourse.mybir as mybir
+from concourse.masks import make_identity
 
 D, T, Q, I, J = 512, 2048, 128, 512, 512
 FLOPS = 2 * D * T * Q
@@ -19,6 +20,10 @@ PACK = 4
 CHUNKS = ((1024, 576, 256, 512), (512, 256, 256, 512), (256, 256, 128, 256), (256, 256, 128, 128))
 FIRST = 128
 QUERY_AT = 2
+BANK = 512
+HALF = 1024
+VEC_COLS = 1664
+OUT_SPLIT = 384
 
 
 def interleave(copy, grouped, raw, lo, hi):
@@ -49,16 +54,22 @@ def tile_attend_evictscores_heads_kernel(tc, query, keys, mass, dec, offs, offs2
         nc.sync.dma_start(slots[:], offs)
         dec_sb = keep.tile([P, 1], F32, name="dec_sb")
         nc.sync.dma_start(out=dec_sb[:], in_=dec)
-        mass_lo = keep.tile([P, T // 2], F32, name="mass_lo", tag="mass_lo_p_first")
-        nc.sync.dma_start(out=mass_lo[:], in_=mass[:, : T // 2])
-        mass_hi = keep.tile([P, T // 2], F32, name="mass_hi")
-        nc.sync.dma_start(out=mass_hi[:], in_=mass[:, T // 2 :])
+        mass_lo = keep.tile([P, HALF], F32, name="mass_lo")
+        nc.sync.dma_start(out=mass_lo[:], in_=mass[:, :HALF])
+        mass_mid = keep.tile([P, VEC_COLS - HALF], F32, name="mass_mid", tag="mass_lo_p_first")
+        nc.sync.dma_start(out=mass_mid[:], in_=mass[:, HALF:VEC_COLS])
+        mass_hi = keep.tile([P, T - VEC_COLS], F32, name="mass_hi")
+        nc.sync.dma_start(out=mass_hi[:], in_=mass[:, VEC_COLS:])
         cands = keep.tile([P, J // 16], U16, name="cands")
         nc.sync.dma_start(cands[:], offs2)
 
 
         placed = keep.tile([P, T], F32, name="placed")
         nc.vector.memset(placed[:], 0.0)
+        twos = keep.tile([P, J], F32, name="twos")
+        nc.gpsimd.memset(twos[:], 2.0)
+        ident = keep.tile([P, P], F32, name="ident")
+        make_identity(nc, ident[:])
 
         q_bf = keep.tile([P, Q, PACK], BF16, name="q_bf", align_bytes=64)
         interleave(nc.vector.tensor_copy, q_bf, q_raw, 0, Q)
@@ -67,6 +78,7 @@ def tile_attend_evictscores_heads_kernel(tc, query, keys, mass, dec, offs, offs2
         nc.vector.quantize_mx(out=q_codes[:].bitcast(FP8X4), scales=q_scales[:], in_=q_bf[:].rearrange("p w j -> p (w j)"))
 
         scores = keep.tile([P, T], F32, name="scores")
+        bank = 0
         t0 = 0
         for c, (width, share, step, n_tile) in enumerate(CHUNKS):
             k_bf = keep.tile([P, width, PACK], BF16, name=f"k_bf{c}", align_bytes=64)
@@ -85,7 +97,8 @@ def tile_attend_evictscores_heads_kernel(tc, query, keys, mass, dec, offs, offs2
                     in_=k_bf[:, lo : lo + step, :].rearrange("p w j -> p (w j)"),
                 )
             for lo in range(0, width, n_tile):
-                acc = psum.tile([Q, n_tile], F32, name=f"acc{c}_{lo}")
+                acc = psum.tile([Q, n_tile], F32, name=f"acc{c}_{lo}", tag=f"bank{bank}")
+                bank = bank + 1
                 nc.tensor.matmul_mx(
                     out=acc[:],
                     lhsT=q_codes[:].bitcast(FP8X4),
@@ -99,8 +112,16 @@ def tile_attend_evictscores_heads_kernel(tc, query, keys, mass, dec, offs, offs2
                 leave(out=scores[:, t0 + lo : t0 + lo + n_tile], in_=acc[:])
             t0 = t0 + width
 
-        decayed_lo = keep.tile([P, T // 2], F32, name="decayed_lo")
-        nc.scalar.activation(out=decayed_lo[:], in_=mass_lo[:], func=ACT.Copy, scale=dec_sb[:])
+        decayed = keep.tile([P, VEC_COLS], F32, name="decayed")
+        nc.scalar.activation(out=decayed[:, :HALF], in_=mass_lo[:], func=ACT.Copy, scale=dec_sb[:])
+        nc.scalar.activation(out=decayed[:, HALF:], in_=mass_mid[:], func=ACT.Copy, scale=dec_sb[:])
+        spans = [(lo, min(lo + BANK, VEC_COLS)) for lo in range(0, VEC_COLS, BANK)]
+        turned_ps = []
+        for b, (lo, hi) in enumerate(spans):
+            turn = psum.tile([P, hi - lo], F32, name=f"turn{b}", tag=f"bank{(6 + b) % 8}")
+            for j in range(lo, hi, P):
+                nc.tensor.transpose(turn[:, j - lo : j - lo + P], decayed[:, j : j + P], ident[:])
+            turned_ps.append(turn)
         listed = keep.tile([P, I], F32, name="listed", tag="listed_decayed")
         nc.vector.tensor_copy(listed[:], scores[:].indirect(slots[:]))
         neg_max = keep.tile([P, 1], F32, name="neg_max")
@@ -117,16 +138,28 @@ def tile_attend_evictscores_heads_kernel(tc, query, keys, mass, dec, offs, offs2
         nc.vector.reciprocal(out=inv_sum[:], in_=p_sum[:])
         nc.vector.tensor_copy(placed[:].indirect(slots[:, FIRST // 16 :]), p_both[:, 2 * FIRST :])
 
-        decayed_hi = keep.tile([P, T // 2], F32, name="decayed_hi", tag="listed_decayed")
-        nc.scalar.activation(out=decayed_hi[:], in_=mass_hi[:], func=ACT.Copy, scale=dec_sb[:])
+        late = keep.tile([P, T], F32, name="late", tag="listed_decayed")
+        decayed_ps = []
+        for b, (lo, hi) in enumerate(spans):
+            nc.scalar.copy(out=late[:, lo:hi], in_=turned_ps[b][:])
+            back = psum.tile([P, hi - lo], F32, name=f"back{b}", tag=f"bank{2 + b}")
+            for j in range(lo, hi, P):
+                nc.tensor.transpose(back[:, j - lo : j - lo + P], late[:, j : j + P], ident[:])
+            decayed_ps.append(back)
+        nc.scalar.activation(out=late[:, VEC_COLS:], in_=mass_hi[:], func=ACT.Copy, scale=dec_sb[:])
         gain = keep.tile([P, 1], F32, name="gain")
         nc.scalar.activation(out=gain[:], in_=inv_sum[:], func=ACT.Copy, scale=512.0)
         updated = keep.tile([P, T], F32, name="updated")
-        for half, decayed in enumerate((decayed_lo, decayed_hi)):
-            cols = slice(half * T // 2, (half + 1) * T // 2)
+        weights_hi = keep.tile([P, T - VEC_COLS], F32, name="weights_hi")
+        nc.gpsimd.tensor_scalar(weights_hi[:], placed[:, VEC_COLS:], gain[:], 0.0, ALU.mult, ALU.add)
+        nc.gpsimd.tensor_tensor(updated[:, VEC_COLS:], weights_hi[:], late[:, VEC_COLS:], ALU.add)
+        for b, (lo, hi) in enumerate(spans):
             nc.vector.scalar_tensor_tensor(
-                out=updated[:, cols], in0=placed[:, cols], scalar=gain[:], in1=decayed[:], op0=ALU.mult, op1=ALU.add
+                out=updated[:, lo:hi], in0=placed[:, lo:hi], scalar=gain[:], in1=decayed_ps[b][:], op0=ALU.mult, op1=ALU.add
             )
-        result = keep.tile([P, J], F32, name="result")
-        nc.vector.tensor_scalar(result[:], updated[:].indirect(cands[:]), 2.0, 0.0, ALU.mult, ALU.add)
-        nc.sync.dma_start(out=out, in_=result[:])
+        for lo, hi in ((0, OUT_SPLIT), (OUT_SPLIT, J)):
+            result = keep.tile([P, hi - lo], F32, name=f"result{lo}")
+            nc.vector.tensor_tensor(
+                result[:], updated[:].indirect(cands[:, lo // 16 : hi // 16]), twos[:, lo:hi], ALU.mult
+            )
+            nc.sync.dma_start(out=out[:, lo:hi], in_=result[:])

@@ -23,7 +23,6 @@ QUERY_AT = 2
 BANK = 512
 HALF = 1024
 VEC_COLS = 1664
-OUT_SPLIT = 384
 
 
 def interleave(copy, grouped, raw, lo, hi):
@@ -66,8 +65,6 @@ def tile_attend_evictscores_heads_kernel(tc, query, keys, mass, dec, offs, offs2
 
         placed = keep.tile([P, T], F32, name="placed")
         nc.vector.memset(placed[:], 0.0)
-        twos = keep.tile([P, J], F32, name="twos")
-        nc.gpsimd.memset(twos[:], 2.0)
         ident = keep.tile([P, P], F32, name="ident")
         make_identity(nc, ident[:])
 
@@ -157,9 +154,6 @@ def tile_attend_evictscores_heads_kernel(tc, query, keys, mass, dec, offs, offs2
             nc.vector.scalar_tensor_tensor(
                 out=updated[:, lo:hi], in0=placed[:, lo:hi], scalar=gain[:], in1=decayed_ps[b][:], op0=ALU.mult, op1=ALU.add
             )
-        for lo, hi in ((0, OUT_SPLIT), (OUT_SPLIT, J)):
-            result = keep.tile([P, hi - lo], F32, name=f"result{lo}")
-            nc.vector.tensor_tensor(
-                result[:], updated[:].indirect(cands[:, lo // 16 : hi // 16]), twos[:, lo:hi], ALU.mult
-            )
-            nc.sync.dma_start(out=out[:, lo:hi], in_=result[:])
+        result = keep.tile([P, J], F32, name="result")
+        nc.vector.tensor_scalar(result[:], updated[:].indirect(cands[:]), 2.0, 0.0, ALU.mult, ALU.add)
+        nc.sync.dma_start(out=out, in_=result[:])

@@ -17,7 +17,7 @@ ACT = mybir.ActivationFunctionType
 
 P = 128
 PACK = 4
-CHUNKS = ((1024, 576, 256, 512), (512, 256, 256, 512), (256, 256, 128, 256), (256, 256, 128, 128))
+CHUNKS = ((1024, 576, (256,) * 4, (512, 512)), (512, 256, (256, 256), (512,)), (256, 256, (128, 128), (256,)), (256, 256, (128, 64, 64), (128, 64, 64)))
 FIRST = 128
 QUERY_AT = 2
 BANK = 512
@@ -42,7 +42,7 @@ def tile_attend_evictscores_heads_kernel(tc, query, keys, mass, dec, offs, offs2
         k_view = keys.rearrange("(p j) t -> p j t", j=PACK)
         k_raw = []
         t0 = 0
-        for c, (width, share, step, n_tile) in enumerate(CHUNKS):
+        for c, (width, share, steps, n_tiles) in enumerate(CHUNKS):
             if c == QUERY_AT:
                 nc.sync.dma_start(out=q_raw[:], in_=query.rearrange("(p j) q -> p j q", j=PACK))
             raw = keep.tile([P, PACK, width], F32, name=f"k_raw{c}")
@@ -77,23 +77,26 @@ def tile_attend_evictscores_heads_kernel(tc, query, keys, mass, dec, offs, offs2
         scores = keep.tile([P, T], F32, name="scores")
         bank = 0
         t0 = 0
-        for c, (width, share, step, n_tile) in enumerate(CHUNKS):
+        for c, (width, share, steps, n_tiles) in enumerate(CHUNKS):
             k_bf = keep.tile([P, width, PACK], BF16, name=f"k_bf{c}", align_bytes=64)
             k_codes = keep.tile([P, width], U32, name=f"k_codes{c}", align_bytes=64)
             k_scales = keep.tile([P, width], U8, name=f"k_scales{c}", align_bytes=64)
-            for lo in range(0, width, step):
+            for s, step in enumerate(steps):
+                lo = sum(steps[:s])
                 hi = lo + step
                 if lo < share:
                     interleave(nc.vector.tensor_copy, k_bf, k_raw[c], lo, min(hi, share))
                 if hi > share:
                     interleave(nc.scalar.copy, k_bf, k_raw[c], max(lo, share), hi)
-            for lo in range(0, width, step):
+            for s, step in enumerate(steps):
+                lo = sum(steps[:s])
                 nc.vector.quantize_mx(
                     out=k_codes[:, lo : lo + step].bitcast(FP8X4),
                     scales=k_scales[:, lo : lo + step],
                     in_=k_bf[:, lo : lo + step, :].rearrange("p w j -> p (w j)"),
                 )
-            for lo in range(0, width, n_tile):
+            for s, n_tile in enumerate(n_tiles):
+                lo = sum(n_tiles[:s])
                 acc = psum.tile([Q, n_tile], F32, name=f"acc{c}_{lo}", tag=f"bank{bank}")
                 bank = bank + 1
                 nc.tensor.matmul_mx(
@@ -115,7 +118,7 @@ def tile_attend_evictscores_heads_kernel(tc, query, keys, mass, dec, offs, offs2
         spans = [(lo, min(lo + BANK, VEC_COLS)) for lo in range(0, VEC_COLS, BANK)]
         turned_ps = []
         for b, (lo, hi) in enumerate(spans):
-            turn = psum.tile([P, hi - lo], F32, name=f"turn{b}", tag=f"bank{(6 + b) % 8}")
+            turn = psum.tile([P, hi - lo], F32, name=f"turn{b}", tag=f"bank{(7 + b) % 8}")
             for j in range(lo, hi, P):
                 nc.tensor.transpose(turn[:, j - lo : j - lo + P], decayed[:, j : j + P], ident[:])
             turned_ps.append(turn)
@@ -139,7 +142,7 @@ def tile_attend_evictscores_heads_kernel(tc, query, keys, mass, dec, offs, offs2
         decayed_ps = []
         for b, (lo, hi) in enumerate(spans):
             nc.scalar.copy(out=late[:, lo:hi], in_=turned_ps[b][:])
-            back = psum.tile([P, hi - lo], F32, name=f"back{b}", tag=f"bank{2 + b}")
+            back = psum.tile([P, hi - lo], F32, name=f"back{b}", tag=f"bank{3 + b}")
             for j in range(lo, hi, P):
                 nc.tensor.transpose(back[:, j - lo : j - lo + P], late[:, j : j + P], ident[:])
             decayed_ps.append(back)

@@ -51,8 +51,10 @@ def tile_attend_evictscores_heads_kernel(tc, query, keys, mass, dec, offs, offs2
             t0 = t0 + width
         slots = keep.tile([P, I // 16], U16, name="slots")
         nc.sync.dma_start(slots[:], offs)
+        dec_raw = keep.tile([P, 1], F32, name="dec_raw")
+        nc.sync.dma_start(out=dec_raw[:], in_=dec)
         dec_sb = keep.tile([P, 1], F32, name="dec_sb")
-        nc.sync.dma_start(out=dec_sb[:], in_=dec)
+        nc.gpsimd.tensor_scalar(dec_sb[:], dec_raw[:], 2.0, 0.0, ALU.mult, ALU.add)
         mass_lo = keep.tile([P, HALF], F32, name="mass_lo")
         nc.sync.dma_start(out=mass_lo[:], in_=mass[:, :HALF])
         mass_mid = keep.tile([P, VEC_COLS - HALF], F32, name="mass_mid", tag="mass_lo_p_first")
@@ -148,7 +150,7 @@ def tile_attend_evictscores_heads_kernel(tc, query, keys, mass, dec, offs, offs2
             decayed_ps.append(back)
         nc.scalar.activation(out=late[:, VEC_COLS:], in_=mass_hi[:], func=ACT.Copy, scale=dec_sb[:])
         gain = keep.tile([P, 1], F32, name="gain")
-        nc.scalar.activation(out=gain[:], in_=inv_sum[:], func=ACT.Copy, scale=512.0)
+        nc.scalar.activation(out=gain[:], in_=inv_sum[:], func=ACT.Copy, scale=1024.0)
         updated = keep.tile([P, T], F32, name="updated")
         weights_hi = keep.tile([P, T - VEC_COLS], F32, name="weights_hi")
         nc.gpsimd.tensor_scalar(weights_hi[:], placed[:, VEC_COLS:], gain[:], 0.0, ALU.mult, ALU.add)
@@ -158,5 +160,7 @@ def tile_attend_evictscores_heads_kernel(tc, query, keys, mass, dec, offs, offs2
                 out=updated[:, lo:hi], in0=placed[:, lo:hi], scalar=gain[:], in1=decayed_ps[b][:], op0=ALU.mult, op1=ALU.add
             )
         result = keep.tile([P, J], F32, name="result")
-        nc.vector.tensor_scalar(result[:], updated[:].indirect(cands[:]), 2.0, 0.0, ALU.mult, ALU.add)
-        nc.sync.dma_start(out=out, in_=result[:])
+        for h in range(2):
+            lo, hi = h * J // 2, (h + 1) * J // 2
+            nc.vector.tensor_copy(result[:, lo:hi].bitcast(U32), updated[:].bitcast(U32).indirect(cands[:, lo // 16 : hi // 16]))
+            nc.sync.dma_start(out=out[:, lo:hi], in_=result[:, lo:hi])

@@ -129,16 +129,15 @@ def tile_attend_evictscores_heads_kernel(tc, query, keys, mass, dec, offs, offs2
         neg_max = keep.tile([P, 1], F32, name="neg_max")
         nc.vector.tensor_reduce(out=neg_max[:], in_=listed[:], axis=mybir.AxisListType.X, op=ALU.max, negate=True)
         p_both = keep.tile([P, FIRST + I], F32, name="p_both", tag="mass_lo_p_first")
-        p_first = p_both[:, :FIRST]
         p_all = p_both[:, FIRST:]
-        nc.scalar.activation(out=p_first, in_=listed[:, :FIRST], func=ACT.Exp, bias=neg_max[:])
         p_sum = keep.tile([P, 1], F32, name="p_sum")
         nc.scalar.activation(out=p_all, in_=listed[:], func=ACT.Exp, bias=neg_max[:], accum_out=p_sum[:])
 
-        nc.vector.tensor_copy(placed[:].indirect(slots[:, : FIRST // 16]), p_first)
         inv_sum = keep.tile([P, 1], F32, name="inv_sum")
-        nc.vector.reciprocal(out=inv_sum[:], in_=p_sum[:])
-        nc.vector.tensor_copy(placed[:].indirect(slots[:, FIRST // 16 :]), p_both[:, 2 * FIRST :])
+        minus_one = keep.tile([P, 1], F32, name="minus_one")
+        nc.gpsimd.memset(minus_one[:], -1.0)
+        nc.gpsimd.tensor_tensor(inv_sum[:], p_sum[:], minus_one[:], ALU.pow)
+        nc.vector.tensor_copy(placed[:].indirect(slots[:]), p_all)
 
         late = keep.tile([P, T], F32, name="late", tag="listed_decayed")
         decayed_ps = []

@@ -17,9 +17,15 @@ ACT = mybir.ActivationFunctionType
 
 P = 128
 PACK = 4
-CHUNKS = ((1024, 576, (256,) * 4, (512, 512)), (512, 256, (256, 256), (512,)), (256, 256, (128, 128), (256,)), (256, 256, (128, 64, 64), (128, 64, 64)))
+CHUNKS = (
+    (0, 1024, ((0, 256, True), (256, 256, True), (512, 256, False), (768, 256, False)), ((0, 256), (256, 256), (512, 256), (768, 256))),
+    (1024, 512, ((0, 256, True), (256, 256, False)), ((0, 256), (256, 256))),
+    (1536, 256, ((0, 128, True), (128, 128, True)), ((0, 128), (128, 128))),
+    (1792, 256, ((0, 128, True), (128, 48, True), (176, 80, False)), ((0, 128), (128, 64), (192, 64))),
+)
+BANKS = ((0, (512,), False), (512, (512,), False), (1024, (256, 256), False), (1536, (256, 128), False), (1920, (64,), True), (1984, (64,), True))
 FIRST = 128
-QUERY_AT = 2
+QUERY_AT = 1
 BANK = 512
 HALF = 1024
 VEC_COLS = 1664
@@ -41,14 +47,12 @@ def tile_attend_evictscores_heads_kernel(tc, query, keys, mass, dec, offs, offs2
         q_raw = keep.tile([P, PACK, Q], F32, name="q_raw")
         k_view = keys.rearrange("(p j) t -> p j t", j=PACK)
         k_raw = []
-        t0 = 0
-        for c, (width, share, steps, n_tiles) in enumerate(CHUNKS):
+        for c, (t0, width, copies, steps) in enumerate(CHUNKS):
             if c == QUERY_AT:
                 nc.sync.dma_start(out=q_raw[:], in_=query.rearrange("(p j) q -> p j q", j=PACK))
-            raw = keep.tile([P, PACK, width], F32, name=f"k_raw{c}")
+            raw = keep.tile([P, PACK, width], F32, name=f"k_raw{c}", tag="scores" if c == 1 else f"k_raw{c}")
             nc.sync.dma_start(out=raw[:], in_=k_view[:, :, t0 : t0 + width])
             k_raw.append(raw)
-            t0 = t0 + width
         slots = keep.tile([P, I // 16], U16, name="slots")
         nc.sync.dma_start(slots[:], offs)
         dec_raw = keep.tile([P, 1], F32, name="dec_raw")
@@ -76,43 +80,36 @@ def tile_attend_evictscores_heads_kernel(tc, query, keys, mass, dec, offs, offs2
         q_scales = keep.tile([P, Q], U8, name="q_scales", align_bytes=64)
         nc.vector.quantize_mx(out=q_codes[:].bitcast(FP8X4), scales=q_scales[:], in_=q_bf[:].rearrange("p w j -> p (w j)"))
 
-        scores = keep.tile([P, T], F32, name="scores")
-        bank = 0
-        t0 = 0
-        for c, (width, share, steps, n_tiles) in enumerate(CHUNKS):
+        k_codes = keep.tile([P, T], U32, name="k_codes", align_bytes=64)
+        k_scales = keep.tile([P, T], U8, name="k_scales", align_bytes=64)
+        for c, (t0, width, copies, steps) in enumerate(CHUNKS):
             k_bf = keep.tile([P, width, PACK], BF16, name=f"k_bf{c}", align_bytes=64)
-            k_codes = keep.tile([P, width], U32, name=f"k_codes{c}", align_bytes=64)
-            k_scales = keep.tile([P, width], U8, name=f"k_scales{c}", align_bytes=64)
-            for s, step in enumerate(steps):
-                lo = sum(steps[:s])
-                hi = lo + step
-                if lo < share:
-                    interleave(nc.vector.tensor_copy, k_bf, k_raw[c], lo, min(hi, share))
-                if hi > share:
-                    interleave(nc.scalar.copy, k_bf, k_raw[c], max(lo, share), hi)
-            for s, step in enumerate(steps):
-                lo = sum(steps[:s])
+            for lo, count, on_vector in copies:
+                interleave(nc.vector.tensor_copy if on_vector else nc.scalar.copy, k_bf, k_raw[c], lo, lo + count)
+            for lo, step in steps:
                 nc.vector.quantize_mx(
-                    out=k_codes[:, lo : lo + step].bitcast(FP8X4),
-                    scales=k_scales[:, lo : lo + step],
+                    out=k_codes[:, t0 + lo : t0 + lo + step].bitcast(FP8X4),
+                    scales=k_scales[:, t0 + lo : t0 + lo + step],
                     in_=k_bf[:, lo : lo + step, :].rearrange("p w j -> p (w j)"),
                 )
-            for s, n_tile in enumerate(n_tiles):
-                lo = sum(n_tiles[:s])
-                acc = psum.tile([Q, n_tile], F32, name=f"acc{c}_{lo}", tag=f"bank{bank}")
-                bank = bank + 1
+
+        scores = keep.tile([P, T], F32, name="scores", tag="scores")
+        for bank, (t0, groups, on_vector) in enumerate(BANKS):
+            width = sum(groups)
+            acc = psum.tile([Q, width], F32, name=f"acc{bank}", tag=f"bank{bank}")
+            for g, n_tile in enumerate(groups):
+                lo = sum(groups[:g])
                 nc.tensor.matmul_mx(
-                    out=acc[:],
+                    out=acc[:, lo : lo + n_tile],
                     lhsT=q_codes[:].bitcast(FP8X4),
                     lhsT_scale=q_scales[:],
-                    rhs=k_codes[:, lo : lo + n_tile].bitcast(FP8X4),
-                    rhs_scale=k_scales[:, lo : lo + n_tile],
+                    rhs=k_codes[:, t0 + lo : t0 + lo + n_tile].bitcast(FP8X4),
+                    rhs_scale=k_scales[:, t0 + lo : t0 + lo + n_tile],
                     start=True,
                     stop=True,
                 )
-                leave = nc.vector.tensor_copy if c == len(CHUNKS) - 1 else nc.scalar.copy
-                leave(out=scores[:, t0 + lo : t0 + lo + n_tile], in_=acc[:])
-            t0 = t0 + width
+            leave = nc.vector.tensor_copy if on_vector else nc.scalar.copy
+            leave(out=scores[:, t0 : t0 + width], in_=acc[:])
 
         decayed = keep.tile([P, VEC_COLS], F32, name="decayed")
         nc.scalar.activation(out=decayed[:, :HALF], in_=mass_lo[:], func=ACT.Copy, scale=dec_sb[:])

@@ -24,10 +24,10 @@ CHUNKS = (
     (1792, 256, ((0, 128, True), (128, 48, True), (176, 80, False)), ((0, 128), (128, 64), (192, 64))),
 )
 BANKS = ((0, (512,), False), (512, (512,), False), (1024, (256, 256), False), (1536, (256, 128), False), (1920, (64,), True), (1984, (64,), True))
-FIRST = 128
 QUERY_AT = 1
 BANK = 512
 HALF = 1024
+EARLY = 1536
 VEC_COLS = 1664
 
 
@@ -53,21 +53,20 @@ def tile_attend_evictscores_heads_kernel(tc, query, keys, mass, dec, offs, offs2
             raw = keep.tile([P, PACK, width], F32, name=f"k_raw{c}", tag="scores" if c == 1 else f"k_raw{c}")
             nc.sync.dma_start(out=raw[:], in_=k_view[:, :, t0 : t0 + width])
             k_raw.append(raw)
+        mass_lo = keep.tile([P, HALF], F32, name="mass_lo")
+        nc.sync.dma_start(out=mass_lo[:], in_=mass[:, :HALF])
         slots = keep.tile([P, I // 16], U16, name="slots")
         nc.sync.dma_start(slots[:], offs)
         dec_raw = keep.tile([P, 1], F32, name="dec_raw")
         nc.sync.dma_start(out=dec_raw[:], in_=dec)
         dec_sb = keep.tile([P, 1], F32, name="dec_sb")
-        nc.gpsimd.tensor_scalar(dec_sb[:], dec_raw[:], 2.0, 0.0, ALU.mult, ALU.add)
-        mass_lo = keep.tile([P, HALF], F32, name="mass_lo")
-        nc.sync.dma_start(out=mass_lo[:], in_=mass[:, :HALF])
-        mass_mid = keep.tile([P, VEC_COLS - HALF], F32, name="mass_mid", tag="mass_lo_p_first")
-        nc.sync.dma_start(out=mass_mid[:], in_=mass[:, HALF:VEC_COLS])
-        mass_hi = keep.tile([P, T - VEC_COLS], F32, name="mass_hi")
-        nc.sync.dma_start(out=mass_hi[:], in_=mass[:, VEC_COLS:])
+        nc.scalar.activation(out=dec_sb[:], in_=dec_raw[:], func=ACT.Copy, scale=2.0)
+        mass_mid = keep.tile([P, EARLY - HALF], F32, name="mass_mid", tag="mass_mid_p")
+        nc.sync.dma_start(out=mass_mid[:], in_=mass[:, HALF:EARLY])
+        mass_hi = keep.tile([P, T - EARLY], F32, name="mass_hi")
+        nc.sync.dma_start(out=mass_hi[:], in_=mass[:, EARLY:])
         cands = keep.tile([P, J // 16], U16, name="cands")
         nc.sync.dma_start(cands[:], offs2)
-
 
         placed = keep.tile([P, T], F32, name="placed")
         nc.vector.memset(placed[:], 0.0)
@@ -111,46 +110,46 @@ def tile_attend_evictscores_heads_kernel(tc, query, keys, mass, dec, offs, offs2
             leave = nc.vector.tensor_copy if on_vector else nc.scalar.copy
             leave(out=scores[:, t0 : t0 + width], in_=acc[:])
 
-        decayed = keep.tile([P, VEC_COLS], F32, name="decayed")
-        nc.scalar.activation(out=decayed[:, :HALF], in_=mass_lo[:], func=ACT.Copy, scale=dec_sb[:])
-        nc.scalar.activation(out=decayed[:, HALF:], in_=mass_mid[:], func=ACT.Copy, scale=dec_sb[:])
-        spans = [(lo, min(lo + BANK, VEC_COLS)) for lo in range(0, VEC_COLS, BANK)]
-        turned_ps = []
-        for b, (lo, hi) in enumerate(spans):
-            turn = psum.tile([P, hi - lo], F32, name=f"turn{b}", tag=f"bank{(7 + b) % 8}")
-            for j in range(lo, hi, P):
-                nc.tensor.transpose(turn[:, j - lo : j - lo + P], decayed[:, j : j + P], ident[:])
-            turned_ps.append(turn)
-        listed = keep.tile([P, I], F32, name="listed", tag="listed_decayed")
+        decayed_lo = keep.tile([P, EARLY], F32, name="decayed_lo")
+        nc.scalar.activation(out=decayed_lo[:, :HALF], in_=mass_lo[:], func=ACT.Copy, scale=dec_sb[:])
+        nc.scalar.activation(out=decayed_lo[:, HALF:], in_=mass_mid[:], func=ACT.Copy, scale=dec_sb[:])
+        listed = keep.tile([P, I], F32, name="listed", tag="listed_late")
         nc.vector.tensor_copy(listed[:], scores[:].indirect(slots[:]))
         neg_max = keep.tile([P, 1], F32, name="neg_max")
         nc.vector.tensor_reduce(out=neg_max[:], in_=listed[:], axis=mybir.AxisListType.X, op=ALU.max, negate=True)
-        p_both = keep.tile([P, FIRST + I], F32, name="p_both", tag="mass_lo_p_first")
-        p_all = p_both[:, FIRST:]
+        p_all = keep.tile([P, I], F32, name="p_all", tag="mass_mid_p")
         p_sum = keep.tile([P, 1], F32, name="p_sum")
-        nc.scalar.activation(out=p_all, in_=listed[:], func=ACT.Exp, bias=neg_max[:], accum_out=p_sum[:])
-
+        nc.scalar.activation(out=p_all[:], in_=listed[:], func=ACT.Exp, bias=neg_max[:], accum_out=p_sum[:])
         inv_sum = keep.tile([P, 1], F32, name="inv_sum")
         minus_one = keep.tile([P, 1], F32, name="minus_one")
         nc.gpsimd.memset(minus_one[:], -1.0)
         nc.gpsimd.tensor_tensor(inv_sum[:], p_sum[:], minus_one[:], ALU.pow)
-        nc.vector.tensor_copy(placed[:].indirect(slots[:]), p_all)
+        nc.vector.tensor_copy(placed[:].indirect(slots[:]), p_all[:])
 
-        late = keep.tile([P, T], F32, name="late", tag="listed_decayed")
+        late = keep.tile([P, VEC_COLS + T - EARLY], F32, name="late", tag="listed_late")
+        decayed_hi = late[:, VEC_COLS:]
+        nc.scalar.activation(out=decayed_hi, in_=mass_hi[:], func=ACT.Copy, scale=dec_sb[:])
+        spans = [(lo, min(lo + BANK, VEC_COLS)) for lo in range(0, VEC_COLS, BANK)]
+        turned = []
+        for b, (lo, hi) in enumerate(spans):
+            turn = psum.tile([P, hi - lo], F32, name=f"turn{b}", tag=f"bank{(7 + b) % 8}")
+            for j in range(lo, hi, P):
+                block = decayed_lo[:, j : j + P] if j < EARLY else decayed_hi[:, j - EARLY : j - EARLY + P]
+                nc.tensor.transpose(turn[:, j - lo : j - lo + P], block, ident[:])
+            turned.append(turn)
         decayed_ps = []
         for b, (lo, hi) in enumerate(spans):
-            nc.scalar.copy(out=late[:, lo:hi], in_=turned_ps[b][:])
+            nc.scalar.copy(out=late[:, lo:hi], in_=turned[b][:])
             back = psum.tile([P, hi - lo], F32, name=f"back{b}", tag=f"bank{3 + b}")
             for j in range(lo, hi, P):
                 nc.tensor.transpose(back[:, j - lo : j - lo + P], late[:, j : j + P], ident[:])
             decayed_ps.append(back)
-        nc.scalar.activation(out=late[:, VEC_COLS:], in_=mass_hi[:], func=ACT.Copy, scale=dec_sb[:])
         gain = keep.tile([P, 1], F32, name="gain")
         nc.scalar.activation(out=gain[:], in_=inv_sum[:], func=ACT.Copy, scale=1024.0)
         updated = keep.tile([P, T], F32, name="updated")
         weights_hi = keep.tile([P, T - VEC_COLS], F32, name="weights_hi")
         nc.gpsimd.tensor_scalar(weights_hi[:], placed[:, VEC_COLS:], gain[:], 0.0, ALU.mult, ALU.add)
-        nc.gpsimd.tensor_tensor(updated[:, VEC_COLS:], weights_hi[:], late[:, VEC_COLS:], ALU.add)
+        nc.gpsimd.tensor_tensor(updated[:, VEC_COLS:], weights_hi[:], decayed_hi[:, VEC_COLS - EARLY :], ALU.add)
         for b, (lo, hi) in enumerate(spans):
             nc.vector.scalar_tensor_tensor(
                 out=updated[:, lo:hi], in0=placed[:, lo:hi], scalar=gain[:], in1=decayed_ps[b][:], op0=ALU.mult, op1=ALU.add

@@ -19,7 +19,7 @@ P = 128
 PACK = 4
 CHUNKS = (
     (0, 1024, ((0, 256, True), (256, 256, True), (512, 256, False), (768, 256, False)), ((0, 256), (256, 256), (512, 256), (768, 256))),
-    (1024, 512, ((0, 256, True), (256, 256, False)), ((0, 256), (256, 256))),
+    (1024, 512, ((0, 256, True), (256, 64, True), (320, 192, False)), ((0, 256), (256, 256))),
     (1536, 256, ((0, 128, True), (128, 128, True)), ((0, 128), (128, 128))),
     (1792, 256, ((0, 128, True), (128, 48, True), (176, 80, False)), ((0, 128), (128, 64), (192, 64))),
 )
@@ -28,6 +28,7 @@ QUERY_AT = 1
 BANK = 512
 HALF = 1024
 EARLY = 1536
+FIRST = 128
 VEC_COLS = 1664
 
 
@@ -117,14 +118,16 @@ def tile_attend_evictscores_heads_kernel(tc, query, keys, mass, dec, offs, offs2
         nc.vector.tensor_copy(listed[:], scores[:].indirect(slots[:]))
         neg_max = keep.tile([P, 1], F32, name="neg_max")
         nc.vector.tensor_reduce(out=neg_max[:], in_=listed[:], axis=mybir.AxisListType.X, op=ALU.max, negate=True)
-        p_all = keep.tile([P, I], F32, name="p_all", tag="mass_mid_p")
+        p_both = keep.tile([P, FIRST + I], F32, name="p_both", tag="mass_mid_p")
+        p_first = p_both[:, :FIRST]
+        p_all = p_both[:, FIRST:]
+        nc.scalar.activation(out=p_first, in_=listed[:, :FIRST], func=ACT.Exp, bias=neg_max[:])
         p_sum = keep.tile([P, 1], F32, name="p_sum")
-        nc.scalar.activation(out=p_all[:], in_=listed[:], func=ACT.Exp, bias=neg_max[:], accum_out=p_sum[:])
+        nc.scalar.activation(out=p_all, in_=listed[:], func=ACT.Exp, bias=neg_max[:], accum_out=p_sum[:])
+        nc.vector.tensor_copy(placed[:].indirect(slots[:, : FIRST // 16]), p_first)
         inv_sum = keep.tile([P, 1], F32, name="inv_sum")
-        minus_one = keep.tile([P, 1], F32, name="minus_one")
-        nc.gpsimd.memset(minus_one[:], -1.0)
-        nc.gpsimd.tensor_tensor(inv_sum[:], p_sum[:], minus_one[:], ALU.pow)
-        nc.vector.tensor_copy(placed[:].indirect(slots[:]), p_all[:])
+        nc.vector.reciprocal(out=inv_sum[:], in_=p_sum[:])
+        nc.vector.tensor_copy(placed[:].indirect(slots[:, FIRST // 16 :]), p_both[:, 2 * FIRST :])
 
         late = keep.tile([P, VEC_COLS + T - EARLY], F32, name="late", tag="listed_late")
         decayed_hi = late[:, VEC_COLS:]

@@ -19,11 +19,12 @@ P = 128
 PACK = 4
 CHUNKS = (
     (0, 1024, ((0, 256, True), (256, 256, True), (512, 256, False), (768, 256, False)), ((0, 256), (256, 256), (512, 256), (768, 256))),
-    (1024, 512, ((0, 256, True), (256, 64, True), (320, 192, False)), ((0, 256), (256, 256))),
+    (1024, 512, ((0, 256, True), (256, 256, False)), ((0, 256), (256, 256))),
     (1536, 256, ((0, 128, True), (128, 128, True)), ((0, 128), (128, 128))),
-    (1792, 256, ((0, 128, True), (128, 48, True), (176, 80, False)), ((0, 128), (128, 64), (192, 64))),
+    (1792, 128, ((0, 128, True),), ((0, 128),)),
+    (1920, 128, ((0, 64, True), (64, 64, True)), ((0, 64), (64, 64))),
 )
-BANKS = ((0, (512,), False), (512, (512,), False), (1024, (256, 256), False), (1536, (256, 128), False), (1920, (64,), True), (1984, (64,), True))
+BANKS = ((0, (512,), False), (512, (512,), False), (1024, (256, 256), False), (1536, (256,), False), (1792, (128,), False), (1920, (64,), True), (1984, (64,), False))
 QUERY_AT = 1
 BANK = 512
 HALF = 1024

@@ -29,7 +29,8 @@ QUERY_AT = 1
 BANK = 512
 HALF = 1024
 EARLY = 1536
-FIRST = 128
+FIRST = 192
+MARGIN = 80.0
 VEC_COLS = 1664
 
 
@@ -55,15 +56,15 @@ def tile_attend_evictscores_heads_kernel(tc, query, keys, mass, dec, offs, offs2
             raw = keep.tile([P, PACK, width], F32, name=f"k_raw{c}", tag="scores" if c == 1 else f"k_raw{c}")
             nc.sync.dma_start(out=raw[:], in_=k_view[:, :, t0 : t0 + width])
             k_raw.append(raw)
-        mass_lo = keep.tile([P, HALF], F32, name="mass_lo")
-        nc.sync.dma_start(out=mass_lo[:], in_=mass[:, :HALF])
         slots = keep.tile([P, I // 16], U16, name="slots")
         nc.sync.dma_start(slots[:], offs)
         dec_raw = keep.tile([P, 1], F32, name="dec_raw")
         nc.sync.dma_start(out=dec_raw[:], in_=dec)
+        mass_lo = keep.tile([P, HALF], F32, name="mass_lo")
+        nc.sync.dma_start(out=mass_lo[:], in_=mass[:, :HALF])
         dec_sb = keep.tile([P, 1], F32, name="dec_sb")
         nc.scalar.activation(out=dec_sb[:], in_=dec_raw[:], func=ACT.Copy, scale=2.0)
-        mass_mid = keep.tile([P, EARLY - HALF], F32, name="mass_mid", tag="mass_mid_p")
+        mass_mid = keep.tile([P, EARLY - HALF], F32, name="mass_mid")
         nc.sync.dma_start(out=mass_mid[:], in_=mass[:, HALF:EARLY])
         mass_hi = keep.tile([P, T - EARLY], F32, name="mass_hi")
         nc.sync.dma_start(out=mass_hi[:], in_=mass[:, EARLY:])
@@ -112,34 +113,36 @@ def tile_attend_evictscores_heads_kernel(tc, query, keys, mass, dec, offs, offs2
             leave = nc.vector.tensor_copy if on_vector else nc.scalar.copy
             leave(out=scores[:, t0 : t0 + width], in_=acc[:])
 
-        decayed_lo = keep.tile([P, EARLY], F32, name="decayed_lo")
-        nc.scalar.activation(out=decayed_lo[:, :HALF], in_=mass_lo[:], func=ACT.Copy, scale=dec_sb[:])
-        nc.scalar.activation(out=decayed_lo[:, HALF:], in_=mass_mid[:], func=ACT.Copy, scale=dec_sb[:])
+        decayed = keep.tile([P, T], F32, name="decayed")
+        for part, lo, hi in ((mass_lo, 0, HALF), (mass_mid, HALF, EARLY), (mass_hi, EARLY, T)):
+            nc.gpsimd.tensor_scalar(decayed[:, lo:hi], part[:], dec_sb[:], 0.0, ALU.mult, ALU.add)
         listed = keep.tile([P, I], F32, name="listed", tag="listed_late")
-        nc.vector.tensor_copy(listed[:], scores[:].indirect(slots[:]))
-        neg_max = keep.tile([P, 1], F32, name="neg_max")
-        nc.vector.tensor_reduce(out=neg_max[:], in_=listed[:], axis=mybir.AxisListType.X, op=ALU.max, negate=True)
-        p_both = keep.tile([P, FIRST + I], F32, name="p_both", tag="mass_mid_p")
+        nc.scalar.activation(out=listed[:], in_=scores[:].indirect(slots[:]), func=ACT.Copy, scale=-1.0)
+        listed_a = keep.tile([P, I // 2], F32, name="listed_a")
+        nc.vector.tensor_copy(listed_a[:].bitcast(U32), scores[:].bitcast(U32).indirect(slots[:, : I // 32]))
+        neg_first = keep.tile([P, 1], F32, name="neg_first")
+        nc.vector.tensor_reduce(out=neg_first[:], in_=listed_a[:], axis=mybir.AxisListType.X, op=ALU.max, negate=True)
+        lowered = keep.tile([P, I // 2], F32, name="lowered")
+        neg_shift = keep.tile([P, 1], F32, name="neg_shift")
+        nc.vector.tensor_scalar(lowered[:], listed[:, I // 2 :], MARGIN, neg_first[:], ALU.add, ALU.min, accum_out=neg_shift[:])
+        p_both = keep.tile([P, FIRST + I], F32, name="p_both")
         p_first = p_both[:, :FIRST]
         p_all = p_both[:, FIRST:]
-        nc.scalar.activation(out=p_first, in_=listed[:, :FIRST], func=ACT.Exp, bias=neg_max[:])
+        nc.scalar.activation(out=p_first, in_=listed_a[:, :FIRST], func=ACT.Exp, bias=neg_first[:])
         p_sum = keep.tile([P, 1], F32, name="p_sum")
-        nc.scalar.activation(out=p_all, in_=listed[:], func=ACT.Exp, bias=neg_max[:], accum_out=p_sum[:])
+        nc.scalar.activation(out=p_all, in_=listed[:], func=ACT.Exp, scale=-1.0, bias=neg_shift[:], accum_out=p_sum[:])
         nc.vector.tensor_copy(placed[:].indirect(slots[:, : FIRST // 16]), p_first)
         inv_sum = keep.tile([P, 1], F32, name="inv_sum")
         nc.vector.reciprocal(out=inv_sum[:], in_=p_sum[:])
         nc.vector.tensor_copy(placed[:].indirect(slots[:, FIRST // 16 :]), p_both[:, 2 * FIRST :])
 
-        late = keep.tile([P, VEC_COLS + T - EARLY], F32, name="late", tag="listed_late")
-        decayed_hi = late[:, VEC_COLS:]
-        nc.scalar.activation(out=decayed_hi, in_=mass_hi[:], func=ACT.Copy, scale=dec_sb[:])
+        late = keep.tile([P, VEC_COLS], F32, name="late", tag="listed_late")
         spans = [(lo, min(lo + BANK, VEC_COLS)) for lo in range(0, VEC_COLS, BANK)]
         turned = []
         for b, (lo, hi) in enumerate(spans):
             turn = psum.tile([P, hi - lo], F32, name=f"turn{b}", tag=f"bank{(7 + b) % 8}")
             for j in range(lo, hi, P):
-                block = decayed_lo[:, j : j + P] if j < EARLY else decayed_hi[:, j - EARLY : j - EARLY + P]
-                nc.tensor.transpose(turn[:, j - lo : j - lo + P], block, ident[:])
+                nc.tensor.transpose(turn[:, j - lo : j - lo + P], decayed[:, j : j + P], ident[:])
             turned.append(turn)
         decayed_ps = []
         for b, (lo, hi) in enumerate(spans):
@@ -153,7 +156,7 @@ def tile_attend_evictscores_heads_kernel(tc, query, keys, mass, dec, offs, offs2
         updated = keep.tile([P, T], F32, name="updated")
         weights_hi = keep.tile([P, T - VEC_COLS], F32, name="weights_hi")
         nc.gpsimd.tensor_scalar(weights_hi[:], placed[:, VEC_COLS:], gain[:], 0.0, ALU.mult, ALU.add)
-        nc.gpsimd.tensor_tensor(updated[:, VEC_COLS:], weights_hi[:], decayed_hi[:, VEC_COLS - EARLY :], ALU.add)
+        nc.gpsimd.tensor_tensor(updated[:, VEC_COLS:], weights_hi[:], decayed[:, VEC_COLS:], ALU.add)
         for b, (lo, hi) in enumerate(spans):
             nc.vector.scalar_tensor_tensor(
                 out=updated[:, lo:hi], in0=placed[:, lo:hi], scalar=gain[:], in1=decayed_ps[b][:], op0=ALU.mult, op1=ALU.add

@@ -36,8 +36,8 @@ VEC_COLS = 1664
 
 def interleave(copy, grouped, raw, lo, hi):
     copy(
-        out=grouped[:, lo:hi, :].rearrange("p (c i) j -> p c j i", i=4),
-        in_=raw[:, :, lo:hi].rearrange("p j (c i) -> p c j i", i=4),
+        out=grouped[:, lo:hi, :].rearrange("p (c i) j -> p c j i", i=2),
+        in_=raw[:, :, lo:hi].rearrange("p j (c i) -> p c j i", i=2),
     )
 
 
@@ -58,12 +58,12 @@ def tile_attend_evictscores_heads_kernel(tc, query, keys, mass, dec, offs, offs2
             k_raw.append(raw)
         slots = keep.tile([P, I // 16], U16, name="slots")
         nc.sync.dma_start(slots[:], offs)
-        dec_raw = keep.tile([P, 1], F32, name="dec_raw")
-        nc.sync.dma_start(out=dec_raw[:], in_=dec)
         mass_lo = keep.tile([P, HALF], F32, name="mass_lo")
         nc.sync.dma_start(out=mass_lo[:], in_=mass[:, :HALF])
+        dec_raw = keep.tile([P, 1], F32, name="dec_raw")
+        nc.sync.dma_start(out=dec_raw[:], in_=dec)
         dec_sb = keep.tile([P, 1], F32, name="dec_sb")
-        nc.scalar.activation(out=dec_sb[:], in_=dec_raw[:], func=ACT.Copy, scale=2.0)
+        nc.gpsimd.tensor_scalar(dec_sb[:], dec_raw[:], 2.0, 0.0, ALU.mult, ALU.add)
         mass_mid = keep.tile([P, EARLY - HALF], F32, name="mass_mid")
         nc.sync.dma_start(out=mass_mid[:], in_=mass[:, HALF:EARLY])
         mass_hi = keep.tile([P, T - EARLY], F32, name="mass_hi")
@@ -116,13 +116,14 @@ def tile_attend_evictscores_heads_kernel(tc, query, keys, mass, dec, offs, offs2
         decayed = keep.tile([P, T], F32, name="decayed")
         for part, lo, hi in ((mass_lo, 0, HALF), (mass_mid, HALF, EARLY), (mass_hi, EARLY, T)):
             nc.gpsimd.tensor_scalar(decayed[:, lo:hi], part[:], dec_sb[:], 0.0, ALU.mult, ALU.add)
-        listed = keep.tile([P, I], F32, name="listed", tag="listed_late")
-        nc.scalar.activation(out=listed[:], in_=scores[:].indirect(slots[:]), func=ACT.Copy, scale=-1.0)
+        listed = keep.tile([P, I + 1], F32, name="listed", tag="listed_late")
+        nc.scalar.activation(out=listed[:, :I], in_=scores[:].indirect(slots[:]), func=ACT.Copy, scale=-1.0)
         listed_a = keep.tile([P, I // 2], F32, name="listed_a")
         nc.vector.tensor_copy(listed_a[:].bitcast(U32), scores[:].bitcast(U32).indirect(slots[:, : I // 32]))
         neg_first = keep.tile([P, 1], F32, name="neg_first")
-        nc.vector.tensor_reduce(out=neg_first[:], in_=listed_a[:], axis=mybir.AxisListType.X, op=ALU.max, negate=True)
-        lowered = keep.tile([P, I // 2], F32, name="lowered")
+        nc.vector.tensor_reduce(out=neg_first[:], in_=listed_a[:, :FIRST], axis=mybir.AxisListType.X, op=ALU.max, negate=True)
+        nc.vector.tensor_reduce(out=listed[:, I:], in_=listed_a[:, FIRST:], axis=mybir.AxisListType.X, op=ALU.max, negate=True)
+        lowered = keep.tile([P, I // 2 + 1], F32, name="lowered")
         neg_shift = keep.tile([P, 1], F32, name="neg_shift")
         nc.vector.tensor_scalar(lowered[:], listed[:, I // 2 :], MARGIN, neg_first[:], ALU.add, ALU.min, accum_out=neg_shift[:])
         p_both = keep.tile([P, FIRST + I], F32, name="p_both")
@@ -130,7 +131,7 @@ def tile_attend_evictscores_heads_kernel(tc, query, keys, mass, dec, offs, offs2
         p_all = p_both[:, FIRST:]
         nc.scalar.activation(out=p_first, in_=listed_a[:, :FIRST], func=ACT.Exp, bias=neg_first[:])
         p_sum = keep.tile([P, 1], F32, name="p_sum")
-        nc.scalar.activation(out=p_all, in_=listed[:], func=ACT.Exp, scale=-1.0, bias=neg_shift[:], accum_out=p_sum[:])
+        nc.scalar.activation(out=p_all, in_=listed[:, :I], func=ACT.Exp, scale=-1.0, bias=neg_shift[:], accum_out=p_sum[:])
         nc.vector.tensor_copy(placed[:].indirect(slots[:, : FIRST // 16]), p_first)
         inv_sum = keep.tile([P, 1], F32, name="inv_sum")
         nc.vector.reciprocal(out=inv_sum[:], in_=p_sum[:])

@@ -24,13 +24,13 @@ CHUNKS = (
     (1792, 128, ((0, 128, True),), ((0, 128),)),
     (1920, 128, ((0, 64, True), (64, 64, True)), ((0, 64), (64, 64))),
 )
-BANKS = ((0, (512,), False), (512, (512,), False), (1024, (256, 256), False), (1536, (256,), False), (1792, (128,), False), (1920, (64,), True), (1984, (64,), False))
+BANKS = ((0, (512,), False), (512, (512,), False), (1024, (256, 256), False), (1536, (256,), False), (1792, (128,), False), (1920, (64,), False), (1984, (64,), False))
 QUERY_AT = 1
 BANK = 512
 HALF = 1024
-EARLY = 1536
 FIRST = 192
 MARGIN = 80.0
+HEAD = 128
 VEC_COLS = 1664
 
 
@@ -59,15 +59,17 @@ def tile_attend_evictscores_heads_kernel(tc, query, keys, mass, dec, offs, offs2
         slots = keep.tile([P, I // 16], U16, name="slots")
         nc.sync.dma_start(slots[:], offs)
         mass_lo = keep.tile([P, HALF], F32, name="mass_lo")
-        nc.sync.dma_start(out=mass_lo[:], in_=mass[:, :HALF])
+        nc.sync.dma_start(out=mass_lo[:], in_=mass[:, HEAD : HEAD + HALF])
         dec_raw = keep.tile([P, 1], F32, name="dec_raw")
         nc.sync.dma_start(out=dec_raw[:], in_=dec)
         dec_sb = keep.tile([P, 1], F32, name="dec_sb")
         nc.gpsimd.tensor_scalar(dec_sb[:], dec_raw[:], 2.0, 0.0, ALU.mult, ALU.add)
-        mass_mid = keep.tile([P, EARLY - HALF], F32, name="mass_mid")
-        nc.sync.dma_start(out=mass_mid[:], in_=mass[:, HALF:EARLY])
-        mass_hi = keep.tile([P, T - EARLY], F32, name="mass_hi")
-        nc.sync.dma_start(out=mass_hi[:], in_=mass[:, EARLY:])
+        mass_head = keep.tile([P, HEAD], F32, name="mass_head", tag="head_p")
+        nc.sync.dma_start(out=mass_head[:], in_=mass[:, :HEAD])
+        mass_mid = keep.tile([P, VEC_COLS - HEAD - HALF], F32, name="mass_mid")
+        nc.sync.dma_start(out=mass_mid[:], in_=mass[:, HEAD + HALF : VEC_COLS])
+        mass_hi = keep.tile([P, T - VEC_COLS], F32, name="mass_hi")
+        nc.sync.dma_start(out=mass_hi[:], in_=mass[:, VEC_COLS:])
         cands = keep.tile([P, J // 16], U16, name="cands")
         nc.sync.dma_start(cands[:], offs2)
 
@@ -114,11 +116,13 @@ def tile_attend_evictscores_heads_kernel(tc, query, keys, mass, dec, offs, offs2
             leave(out=scores[:, t0 : t0 + width], in_=acc[:])
 
         decayed = keep.tile([P, T], F32, name="decayed")
-        for part, lo, hi in ((mass_lo, 0, HALF), (mass_mid, HALF, EARLY), (mass_hi, EARLY, T)):
-            nc.gpsimd.tensor_scalar(decayed[:, lo:hi], part[:], dec_sb[:], 0.0, ALU.mult, ALU.add)
+        updated = keep.tile([P, T], F32, name="updated")
+        nc.gpsimd.tensor_scalar(decayed[:, HEAD : HEAD + HALF], mass_lo[:], dec_sb[:], 0.0, ALU.mult, ALU.add)
+        nc.gpsimd.tensor_scalar(decayed[:, HEAD + HALF : VEC_COLS], mass_mid[:], dec_sb[:], 0.0, ALU.mult, ALU.add)
+        nc.gpsimd.tensor_scalar(decayed[:, VEC_COLS:], mass_hi[:], dec_sb[:], 0.0, ALU.mult, ALU.add)
         listed = keep.tile([P, I + 1], F32, name="listed", tag="listed_late")
         nc.scalar.activation(out=listed[:, :I], in_=scores[:].indirect(slots[:]), func=ACT.Copy, scale=-1.0)
-        listed_a = keep.tile([P, I // 2], F32, name="listed_a")
+        listed_a = keep.tile([P, I // 2], F32, name="listed_a", tag="listed_a")
         nc.vector.tensor_copy(listed_a[:].bitcast(U32), scores[:].bitcast(U32).indirect(slots[:, : I // 32]))
         neg_first = keep.tile([P, 1], F32, name="neg_first")
         nc.vector.tensor_reduce(out=neg_first[:], in_=listed_a[:, :FIRST], axis=mybir.AxisListType.X, op=ALU.max, negate=True)
@@ -126,38 +130,42 @@ def tile_attend_evictscores_heads_kernel(tc, query, keys, mass, dec, offs, offs2
         lowered = keep.tile([P, I // 2 + 1], F32, name="lowered")
         neg_shift = keep.tile([P, 1], F32, name="neg_shift")
         nc.vector.tensor_scalar(lowered[:], listed[:, I // 2 :], MARGIN, neg_first[:], ALU.add, ALU.min, accum_out=neg_shift[:])
-        p_both = keep.tile([P, FIRST + I], F32, name="p_both")
-        p_first = p_both[:, :FIRST]
-        p_all = p_both[:, FIRST:]
-        nc.scalar.activation(out=p_first, in_=listed_a[:, :FIRST], func=ACT.Exp, bias=neg_first[:])
+        p_first = keep.tile([P, FIRST], F32, name="p_first")
+        nc.scalar.activation(out=p_first[:], in_=listed_a[:, :FIRST], func=ACT.Exp, bias=neg_first[:])
+        decayed_head = keep.tile([P, HEAD], F32, name="decayed_head", tag="listed_a")
+        nc.scalar.activation(out=decayed_head[:], in_=mass_head[:], func=ACT.Copy, scale=dec_sb[:])
+        p_all = keep.tile([P, I], F32, name="p_all", tag="head_p")
         p_sum = keep.tile([P, 1], F32, name="p_sum")
-        nc.scalar.activation(out=p_all, in_=listed[:, :I], func=ACT.Exp, scale=-1.0, bias=neg_shift[:], accum_out=p_sum[:])
-        nc.vector.tensor_copy(placed[:].indirect(slots[:, : FIRST // 16]), p_first)
+        nc.scalar.activation(out=p_all[:], in_=listed[:, :I], func=ACT.Exp, scale=-1.0, bias=neg_shift[:], accum_out=p_sum[:])
+        nc.vector.tensor_copy(placed[:].indirect(slots[:, : FIRST // 16]), p_first[:])
         inv_sum = keep.tile([P, 1], F32, name="inv_sum")
         nc.vector.reciprocal(out=inv_sum[:], in_=p_sum[:])
-        nc.vector.tensor_copy(placed[:].indirect(slots[:, FIRST // 16 :]), p_both[:, 2 * FIRST :])
+        nc.vector.tensor_copy(placed[:].indirect(slots[:, FIRST // 16 :]), p_all[:, FIRST:])
 
-        late = keep.tile([P, VEC_COLS], F32, name="late", tag="listed_late")
-        spans = [(lo, min(lo + BANK, VEC_COLS)) for lo in range(0, VEC_COLS, BANK)]
+        gain = keep.tile([P, 1], F32, name="gain")
+        nc.vector.tensor_scalar(gain[:], inv_sum[:], 1024.0, None, ALU.mult)
+
+        late = keep.tile([P, VEC_COLS - HEAD], F32, name="late", tag="listed_late")
+        spans = [(lo, lo + BANK) for lo in range(HEAD, VEC_COLS, BANK)]
         turned = []
         for b, (lo, hi) in enumerate(spans):
-            turn = psum.tile([P, hi - lo], F32, name=f"turn{b}", tag=f"bank{(7 + b) % 8}")
+            turn = psum.tile([P, BANK], F32, name=f"turn{b}", tag=f"bank{(7 + b) % 8}")
             for j in range(lo, hi, P):
                 nc.tensor.transpose(turn[:, j - lo : j - lo + P], decayed[:, j : j + P], ident[:])
             turned.append(turn)
         decayed_ps = []
         for b, (lo, hi) in enumerate(spans):
-            nc.scalar.copy(out=late[:, lo:hi], in_=turned[b][:])
-            back = psum.tile([P, hi - lo], F32, name=f"back{b}", tag=f"bank{3 + b}")
+            nc.scalar.copy(out=late[:, lo - HEAD : hi - HEAD], in_=turned[b][:])
+            back = psum.tile([P, BANK], F32, name=f"back{b}", tag=f"bank{3 + b}")
             for j in range(lo, hi, P):
-                nc.tensor.transpose(back[:, j - lo : j - lo + P], late[:, j : j + P], ident[:])
+                nc.tensor.transpose(back[:, j - lo : j - lo + P], late[:, j - HEAD : j - HEAD + P], ident[:])
             decayed_ps.append(back)
-        gain = keep.tile([P, 1], F32, name="gain")
-        nc.scalar.activation(out=gain[:], in_=inv_sum[:], func=ACT.Copy, scale=1024.0)
-        updated = keep.tile([P, T], F32, name="updated")
         weights_hi = keep.tile([P, T - VEC_COLS], F32, name="weights_hi")
         nc.gpsimd.tensor_scalar(weights_hi[:], placed[:, VEC_COLS:], gain[:], 0.0, ALU.mult, ALU.add)
         nc.gpsimd.tensor_tensor(updated[:, VEC_COLS:], weights_hi[:], decayed[:, VEC_COLS:], ALU.add)
+        nc.vector.scalar_tensor_tensor(
+            out=updated[:, :HEAD], in0=placed[:, :HEAD], scalar=gain[:], in1=decayed_head[:], op0=ALU.mult, op1=ALU.add
+        )
         for b, (lo, hi) in enumerate(spans):
             nc.vector.scalar_tensor_tensor(
                 out=updated[:, lo:hi], in0=placed[:, lo:hi], scalar=gain[:], in1=decayed_ps[b][:], op0=ALU.mult, op1=ALU.add

@@ -18,20 +18,21 @@ ACT = mybir.ActivationFunctionType
 P = 128
 PACK = 4
 CHUNKS = (
-    (0, 1024, ((0, 256, True), (256, 256, True), (512, 256, False), (768, 256, False)), ((0, 256), (256, 256), (512, 256), (768, 256))),
+    (0, 1024, ((0, 512, True), (512, 256, False), (768, 256, False)), ((0, 512), (512, 256), (768, 256))),
     (1024, 512, ((0, 256, True), (256, 256, False)), ((0, 256), (256, 256))),
     (1536, 256, ((0, 128, True), (128, 128, True)), ((0, 128), (128, 128))),
     (1792, 128, ((0, 128, True),), ((0, 128),)),
     (1920, 128, ((0, 64, True), (64, 64, True)), ((0, 64), (64, 64))),
 )
-BANKS = ((0, (512,), False), (512, (512,), False), (1024, (256, 256), False), (1536, (256,), False), (1792, (128,), False), (1920, (64,), False), (1984, (64,), False))
+BANKS = ((0, (512,), False), (512, (512,), False), (1024, (256, 256), False), (1536, (256,), False), (1792, (128,), False), (1920, (64,), True), (1984, (64,), False))
 QUERY_AT = 1
 BANK = 512
 HALF = 1024
-FIRST = 192
+FIRST = 160
 MARGIN = 80.0
-HEAD = 128
-VEC_COLS = 1664
+HEAD = 64
+VEC_COLS = 1600
+OWN = 128
 
 
 def interleave(copy, grouped, raw, lo, hi):
@@ -146,23 +147,27 @@ def tile_attend_evictscores_heads_kernel(tc, query, keys, mass, dec, offs, offs2
         nc.vector.tensor_scalar(gain[:], inv_sum[:], 1024.0, None, ALU.mult)
 
         late = keep.tile([P, VEC_COLS - HEAD], F32, name="late", tag="listed_late")
-        spans = [(lo, lo + BANK) for lo in range(HEAD, VEC_COLS, BANK)]
+        spans = [(lo, min(lo + BANK, VEC_COLS)) for lo in range(HEAD, VEC_COLS, BANK)]
         turned = []
         for b, (lo, hi) in enumerate(spans):
-            turn = psum.tile([P, BANK], F32, name=f"turn{b}", tag=f"bank{(7 + b) % 8}")
+            turn = psum.tile([P, hi - lo], F32, name=f"turn{b}", tag=f"bank{(7 + b) % 8}")
             for j in range(lo, hi, P):
                 nc.tensor.transpose(turn[:, j - lo : j - lo + P], decayed[:, j : j + P], ident[:])
             turned.append(turn)
         decayed_ps = []
         for b, (lo, hi) in enumerate(spans):
             nc.scalar.copy(out=late[:, lo - HEAD : hi - HEAD], in_=turned[b][:])
-            back = psum.tile([P, BANK], F32, name=f"back{b}", tag=f"bank{3 + b}")
+            back = psum.tile([P, hi - lo], F32, name=f"back{b}", tag=f"bank{3 + b}")
             for j in range(lo, hi, P):
                 nc.tensor.transpose(back[:, j - lo : j - lo + P], late[:, j - HEAD : j - HEAD + P], ident[:])
             decayed_ps.append(back)
-        weights_hi = keep.tile([P, T - VEC_COLS], F32, name="weights_hi")
-        nc.gpsimd.tensor_scalar(weights_hi[:], placed[:, VEC_COLS:], gain[:], 0.0, ALU.mult, ALU.add)
-        nc.gpsimd.tensor_tensor(updated[:, VEC_COLS:], weights_hi[:], decayed[:, VEC_COLS:], ALU.add)
+        split = VEC_COLS + OWN
+        weights_own = keep.tile([P, OWN], F32, name="weights_own")
+        nc.gpsimd.tensor_scalar(weights_own[:], placed[:, VEC_COLS:split], gain[:], 0.0, ALU.mult, ALU.add)
+        weights_rest = keep.tile([P, T - split], F32, name="weights_rest", tag="listed_late")
+        nc.scalar.activation(out=weights_rest[:], in_=placed[:, split:], func=ACT.Copy, scale=gain[:])
+        nc.gpsimd.tensor_tensor(updated[:, VEC_COLS:split], weights_own[:], decayed[:, VEC_COLS:split], ALU.add)
+        nc.gpsimd.tensor_tensor(updated[:, split:], weights_rest[:], decayed[:, split:], ALU.add)
         nc.vector.scalar_tensor_tensor(
             out=updated[:, :HEAD], in0=placed[:, :HEAD], scalar=gain[:], in1=decayed_head[:], op0=ALU.mult, op1=ALU.add
         )

@@ -27,7 +27,6 @@ CHUNKS = (
 BANKS = ((0, (512,), False), (512, (512,), False), (1024, (256, 256), False), (1536, (256,), False), (1792, (128,), False), (1920, (64,), True), (1984, (64,), False))
 QUERY_AT = 1
 BANK = 512
-HALF = 1024
 FIRST = 160
 MARGIN = 80.0
 HEAD = 64
@@ -59,16 +58,15 @@ def tile_attend_evictscores_heads_kernel(tc, query, keys, mass, dec, offs, offs2
             k_raw.append(raw)
         slots = keep.tile([P, I // 16], U16, name="slots")
         nc.sync.dma_start(slots[:], offs)
-        mass_lo = keep.tile([P, HALF], F32, name="mass_lo")
-        nc.sync.dma_start(out=mass_lo[:], in_=mass[:, HEAD : HEAD + HALF])
         dec_raw = keep.tile([P, 1], F32, name="dec_raw")
         nc.sync.dma_start(out=dec_raw[:], in_=dec)
-        dec_sb = keep.tile([P, 1], F32, name="dec_sb")
-        nc.gpsimd.tensor_scalar(dec_sb[:], dec_raw[:], 2.0, 0.0, ALU.mult, ALU.add)
+        mass_banks = []
+        for lo in range(HEAD, VEC_COLS, BANK):
+            part = keep.tile([P, BANK], F32, name=f"mass{lo}")
+            nc.sync.dma_start(out=part[:], in_=mass[:, lo : lo + BANK])
+            mass_banks.append(part)
         mass_head = keep.tile([P, HEAD], F32, name="mass_head", tag="head_p")
         nc.sync.dma_start(out=mass_head[:], in_=mass[:, :HEAD])
-        mass_mid = keep.tile([P, VEC_COLS - HEAD - HALF], F32, name="mass_mid")
-        nc.sync.dma_start(out=mass_mid[:], in_=mass[:, HEAD + HALF : VEC_COLS])
         mass_hi = keep.tile([P, T - VEC_COLS], F32, name="mass_hi")
         nc.sync.dma_start(out=mass_hi[:], in_=mass[:, VEC_COLS:])
         cands = keep.tile([P, J // 16], U16, name="cands")
@@ -88,7 +86,7 @@ def tile_attend_evictscores_heads_kernel(tc, query, keys, mass, dec, offs, offs2
         k_codes = keep.tile([P, T], U32, name="k_codes", align_bytes=64)
         k_scales = keep.tile([P, T], U8, name="k_scales", align_bytes=64)
         for c, (t0, width, copies, steps) in enumerate(CHUNKS):
-            k_bf = keep.tile([P, width, PACK], BF16, name=f"k_bf{c}", align_bytes=64)
+            k_bf = keep.tile([P, width, PACK], BF16, name=f"k_bf{c}", tag=f"k_bf{c}", align_bytes=64)
             for lo, count, on_vector in copies:
                 interleave(nc.vector.tensor_copy if on_vector else nc.scalar.copy, k_bf, k_raw[c], lo, lo + count)
             for lo, step in steps:
@@ -116,10 +114,13 @@ def tile_attend_evictscores_heads_kernel(tc, query, keys, mass, dec, offs, offs2
             leave = nc.vector.tensor_copy if on_vector else nc.scalar.copy
             leave(out=scores[:, t0 : t0 + width], in_=acc[:])
 
+        dec_sb = keep.tile([P, 1], F32, name="dec_sb", tag=f"k_bf{len(CHUNKS) - 1}", align_bytes=64)
+        nc.gpsimd.tensor_scalar(dec_sb[:], dec_raw[:], 2.0, 0.0, ALU.mult, ALU.add)
         decayed = keep.tile([P, T], F32, name="decayed")
         updated = keep.tile([P, T], F32, name="updated")
-        nc.gpsimd.tensor_scalar(decayed[:, HEAD : HEAD + HALF], mass_lo[:], dec_sb[:], 0.0, ALU.mult, ALU.add)
-        nc.gpsimd.tensor_scalar(decayed[:, HEAD + HALF : VEC_COLS], mass_mid[:], dec_sb[:], 0.0, ALU.mult, ALU.add)
+        for b, part in enumerate(mass_banks):
+            lo = HEAD + b * BANK
+            nc.gpsimd.tensor_scalar(decayed[:, lo : lo + BANK], part[:], dec_sb[:], 0.0, ALU.mult, ALU.add)
         nc.gpsimd.tensor_scalar(decayed[:, VEC_COLS:], mass_hi[:], dec_sb[:], 0.0, ALU.mult, ALU.add)
         listed = keep.tile([P, I + 1], F32, name="listed", tag="listed_late")
         nc.scalar.activation(out=listed[:, :I], in_=scores[:].indirect(slots[:]), func=ACT.Copy, scale=-1.0)

@@ -17,15 +17,9 @@ ACT = mybir.ActivationFunctionType
 
 P = 128
 PACK = 4
-CHUNKS = (
-    (0, 1024, ((0, 512, True), (512, 256, False), (768, 256, False)), ((0, 512), (512, 256), (768, 256))),
-    (1024, 512, ((0, 256, True), (256, 256, False)), ((0, 256), (256, 256))),
-    (1536, 256, ((0, 128, True), (128, 128, True)), ((0, 128), (128, 128))),
-    (1792, 128, ((0, 128, True),), ((0, 128),)),
-    (1920, 128, ((0, 64, True), (64, 64, True)), ((0, 64), (64, 64))),
-)
-BANKS = ((0, (512,), False), (512, (512,), False), (1024, (256, 256), False), (1536, (256,), False), (1792, (128,), False), (1920, (64,), True), (1984, (64,), False))
-QUERY_AT = 1
+HALF = T // 2
+TAIL = 1536
+LATE_LOADS = ((1536, 256), (1792, 128), (1920, 128))
 BANK = 512
 FIRST = 160
 MARGIN = 80.0
@@ -34,10 +28,10 @@ VEC_COLS = 1600
 OWN = 128
 
 
-def interleave(copy, grouped, raw, lo, hi):
+def interleave(copy, grouped, raw):
     copy(
-        out=grouped[:, lo:hi, :].rearrange("p (c i) j -> p c j i", i=2),
-        in_=raw[:, :, lo:hi].rearrange("p j (c i) -> p c j i", i=2),
+        out=grouped.rearrange("p (c i) (h l) -> p c h l i", i=2, l=2),
+        in_=raw.rearrange("p h l (c i) -> p c h l i", i=2),
     )
 
 
@@ -47,15 +41,18 @@ def tile_attend_evictscores_heads_kernel(tc, query, keys, mass, dec, offs, offs2
         keep = ctx.enter_context(tc.tile_pool(name="keep", bufs=1))
         psum = ctx.enter_context(tc.psum_pool(name="psum", bufs=1))
 
-        q_raw = keep.tile([P, PACK, Q], F32, name="q_raw")
-        k_view = keys.rearrange("(p j) t -> p j t", j=PACK)
-        k_raw = []
-        for c, (t0, width, copies, steps) in enumerate(CHUNKS):
-            if c == QUERY_AT:
-                nc.sync.dma_start(out=q_raw[:], in_=query.rearrange("(p j) q -> p j q", j=PACK))
-            raw = keep.tile([P, PACK, width], F32, name=f"k_raw{c}", tag="scores" if c == 1 else f"k_raw{c}")
-            nc.sync.dma_start(out=raw[:], in_=k_view[:, :, t0 : t0 + width])
-            k_raw.append(raw)
+        k_view = keys.rearrange("(p h l) t -> p h l t", h=2, l=2)
+        first_raw = keep.tile([P, 2, 2, HALF], F32, name="first_raw")
+        nc.sync.dma_start(out=first_raw[:], in_=k_view[:, :, :, :HALF])
+        q_raw = keep.tile([P, 2, 2, Q], F32, name="q_raw")
+        nc.sync.dma_start(out=q_raw[:], in_=query.rearrange("(p h l) q -> p h l q", h=2, l=2))
+        second_raw = keep.tile([P, 2, 2, TAIL - HALF], F32, name="second_raw", tag="scores", align_bytes=64)
+        nc.sync.dma_start(out=second_raw[:], in_=k_view[:, :, :, HALF:TAIL])
+        late_raw = []
+        for lo, width in LATE_LOADS:
+            raw = keep.tile([P, 2, 2, width], F32, name=f"late_raw{lo}")
+            nc.sync.dma_start(out=raw[:], in_=k_view[:, :, :, lo : lo + width])
+            late_raw.append(raw)
         slots = keep.tile([P, I // 16], U16, name="slots")
         nc.sync.dma_start(slots[:], offs)
         dec_raw = keep.tile([P, 1], F32, name="dec_raw")
@@ -78,43 +75,82 @@ def tile_attend_evictscores_heads_kernel(tc, query, keys, mass, dec, offs, offs2
         make_identity(nc, ident[:])
 
         q_bf = keep.tile([P, Q, PACK], BF16, name="q_bf", align_bytes=64)
-        interleave(nc.vector.tensor_copy, q_bf, q_raw, 0, Q)
         q_codes = keep.tile([P, Q], U32, name="q_codes", align_bytes=64)
         q_scales = keep.tile([P, Q], U8, name="q_scales", align_bytes=64)
-        nc.vector.quantize_mx(out=q_codes[:].bitcast(FP8X4), scales=q_scales[:], in_=q_bf[:].rearrange("p w j -> p (w j)"))
-
         k_codes = keep.tile([P, T], U32, name="k_codes", align_bytes=64)
         k_scales = keep.tile([P, T], U8, name="k_scales", align_bytes=64)
-        for c, (t0, width, copies, steps) in enumerate(CHUNKS):
-            k_bf = keep.tile([P, width, PACK], BF16, name=f"k_bf{c}", tag=f"k_bf{c}", align_bytes=64)
-            for lo, count, on_vector in copies:
-                interleave(nc.vector.tensor_copy if on_vector else nc.scalar.copy, k_bf, k_raw[c], lo, lo + count)
-            for lo, step in steps:
-                nc.vector.quantize_mx(
-                    out=k_codes[:, t0 + lo : t0 + lo + step].bitcast(FP8X4),
-                    scales=k_scales[:, t0 + lo : t0 + lo + step],
-                    in_=k_bf[:, lo : lo + step, :].rearrange("p w j -> p (w j)"),
-                )
+        on_vector, on_scalar = nc.vector.tensor_copy, nc.scalar.copy
+        staged = {}
 
-        scores = keep.tile([P, T], F32, name="scores", tag="scores")
-        for bank, (t0, groups, on_vector) in enumerate(BANKS):
-            width = sum(groups)
-            acc = psum.tile([Q, width], F32, name=f"acc{bank}", tag=f"bank{bank}")
-            for g, n_tile in enumerate(groups):
-                lo = sum(groups[:g])
+        def stage(copy, lo, hi, into=None):
+            if lo < HALF:
+                raw = first_raw[:, :, :, lo:hi]
+            elif lo < TAIL:
+                raw = second_raw[:, :, :, lo - HALF : hi - HALF]
+            else:
+                c = max(n for n, (t0, width) in enumerate(LATE_LOADS) if t0 <= lo)
+                raw = late_raw[c][:, :, :, lo - LATE_LOADS[c][0] : hi - LATE_LOADS[c][0]]
+            if into is None:
+                into = keep.tile([P, hi - lo, PACK], BF16, name=f"staged{lo}", tag=f"staged{lo}", align_bytes=64)[:]
+            staged[lo] = into
+            interleave(copy, into, raw)
+
+        def quantise(lo, hi):
+            nc.vector.quantize_mx(
+                out=k_codes[:, lo:hi].bitcast(FP8X4), scales=k_scales[:, lo:hi], in_=staged[lo].rearrange("p w j -> p (w j)")
+            )
+
+        def product(bank, lo, groups):
+            acc = psum.tile([Q, sum(groups)], F32, name=f"acc{lo}", tag=f"bank{bank}")
+            at = 0
+            for n in groups:
                 nc.tensor.matmul_mx(
-                    out=acc[:, lo : lo + n_tile],
+                    out=acc[:, at : at + n],
                     lhsT=q_codes[:].bitcast(FP8X4),
                     lhsT_scale=q_scales[:],
-                    rhs=k_codes[:, t0 + lo : t0 + lo + n_tile].bitcast(FP8X4),
-                    rhs_scale=k_scales[:, t0 + lo : t0 + lo + n_tile],
+                    rhs=k_codes[:, lo + at : lo + at + n].bitcast(FP8X4),
+                    rhs_scale=k_scales[:, lo + at : lo + at + n],
                     start=True,
                     stop=True,
                 )
-            leave = nc.vector.tensor_copy if on_vector else nc.scalar.copy
-            leave(out=scores[:, t0 : t0 + width], in_=acc[:])
+                at += n
+            return acc
 
-        dec_sb = keep.tile([P, 1], F32, name="dec_sb", tag=f"k_bf{len(CHUNKS) - 1}", align_bytes=64)
+        def leave(copy, acc, lo):
+            copy(out=scores[:, lo : lo + acc.shape[1]], in_=acc[:])
+
+        stage(on_vector, 0, 512)
+        interleave(on_vector, q_bf[:], q_raw[:])
+        stage(on_scalar, 512, 768)
+        stage(on_scalar, 768, 1024)
+        quantise(0, 512)
+        nc.vector.quantize_mx(out=q_codes[:].bitcast(FP8X4), scales=q_scales[:], in_=q_bf[:].rearrange("p w j -> p (w j)"))
+        quantise(512, 768)
+        quantise(768, 1024)
+        stage(on_vector, 1024, 1280)
+        stage(on_scalar, 1280, 1536)
+        quantise(1024, 1280)
+        quantise(1280, 1536)
+        stage(on_vector, 1536, 1664)
+        stage(on_vector, 1664, 1792)
+        quantise(1536, 1664)
+        quantise(1664, 1792)
+        stage(on_vector, 1792, 1920)
+        quantise(1792, 1920)
+        scores = keep.tile([P, T], F32, name="scores", tag="scores", align_bytes=64)
+        stage(on_vector, 1920, 1984, scores[:, 1536:1664].bitcast(BF16).rearrange("p (w j) -> p w j", j=PACK))
+        stage(on_vector, 1984, 2048)
+        quantise(1920, 1984)
+        quantise(1984, 2048)
+        leave(on_scalar, product(0, 0, (512,)), 0)
+        leave(on_scalar, product(1, 512, (256, 256)), 512)
+        leave(on_scalar, product(2, 1024, (256, 256)), 1024)
+        leave(on_vector, product(3, 1536, (256,)), 1536)
+        leave(on_scalar, product(4, 1792, (128,)), 1792)
+        leave(on_vector, product(5, 1920, (64,)), 1920)
+        leave(on_scalar, product(6, 1984, (64,)), 1984)
+
+        dec_sb = keep.tile([P, 1], F32, name="dec_sb", tag="staged1984", align_bytes=64)
         nc.gpsimd.tensor_scalar(dec_sb[:], dec_raw[:], 2.0, 0.0, ALU.mult, ALU.add)
         decayed = keep.tile([P, T], F32, name="decayed")
         updated = keep.tile([P, T], F32, name="updated")

@@ -139,7 +139,7 @@ def tile_attend_evictscores_heads_kernel(tc, query, keys, mass, dec, offs, offs2
         quantise(1792, 1920)
         scores = keep.tile([P, T], F32, name="scores", tag="scores", align_bytes=64)
         stage(on_vector, 1920, 1984, scores[:, 1536:1664].bitcast(BF16).rearrange("p (w j) -> p w j", j=PACK))
-        stage(on_vector, 1984, 2048)
+        stage(on_scalar, 1984, 2048)
         quantise(1920, 1984)
         quantise(1984, 2048)
         leave(on_scalar, product(0, 0, (512,)), 0)

@@ -42,15 +42,15 @@ def tile_attend_evictscores_heads_kernel(tc, query, keys, mass, dec, offs, offs2
         psum = ctx.enter_context(tc.psum_pool(name="psum", bufs=1))
 
         k_view = keys.rearrange("(p h l) t -> p h l t", h=2, l=2)
-        first_raw = keep.tile([P, 2, 2, HALF], F32, name="first_raw")
+        first_raw = keep.tile([P, 2, 2, HALF], F32, name="first_raw", align_bytes=256)
         nc.sync.dma_start(out=first_raw[:], in_=k_view[:, :, :, :HALF])
-        q_raw = keep.tile([P, 2, 2, Q], F32, name="q_raw")
+        q_raw = keep.tile([P, 2, 2, Q], F32, name="q_raw", align_bytes=256)
         nc.sync.dma_start(out=q_raw[:], in_=query.rearrange("(p h l) q -> p h l q", h=2, l=2))
-        second_raw = keep.tile([P, 2, 2, TAIL - HALF], F32, name="second_raw", tag="scores", align_bytes=64)
+        second_raw = keep.tile([P, 2, 2, TAIL - HALF], F32, name="second_raw", tag="scores", align_bytes=256)
         nc.sync.dma_start(out=second_raw[:], in_=k_view[:, :, :, HALF:TAIL])
         late_raw = []
         for lo, width in LATE_LOADS:
-            raw = keep.tile([P, 2, 2, width], F32, name=f"late_raw{lo}")
+            raw = keep.tile([P, 2, 2, width], F32, name=f"late_raw{lo}", align_bytes=256)
             nc.sync.dma_start(out=raw[:], in_=k_view[:, :, :, lo : lo + width])
             late_raw.append(raw)
         slots = keep.tile([P, I // 16], U16, name="slots")
@@ -59,7 +59,7 @@ def tile_attend_evictscores_heads_kernel(tc, query, keys, mass, dec, offs, offs2
         nc.sync.dma_start(out=dec_raw[:], in_=dec)
         mass_banks = []
         for lo in range(HEAD, VEC_COLS, BANK):
-            part = keep.tile([P, BANK], F32, name=f"mass{lo}")
+            part = keep.tile([P, BANK], F32, name=f"mass{lo}", align_bytes=256)
             nc.sync.dma_start(out=part[:], in_=mass[:, lo : lo + BANK])
             mass_banks.append(part)
         mass_head = keep.tile([P, HEAD], F32, name="mass_head", tag="head_p")
@@ -137,7 +137,7 @@ def tile_attend_evictscores_heads_kernel(tc, query, keys, mass, dec, offs, offs2
         quantise(1664, 1792)
         stage(on_vector, 1792, 1920)
         quantise(1792, 1920)
-        scores = keep.tile([P, T], F32, name="scores", tag="scores", align_bytes=64)
+        scores = keep.tile([P, T], F32, name="scores", tag="scores", align_bytes=256)
         stage(on_vector, 1920, 1984, scores[:, 1536:1664].bitcast(BF16).rearrange("p (w j) -> p w j", j=PACK))
         stage(on_scalar, 1984, 2048)
         quantise(1920, 1984)
@@ -212,7 +212,7 @@ def tile_attend_evictscores_heads_kernel(tc, query, keys, mass, dec, offs, offs2
             nc.vector.scalar_tensor_tensor(
                 out=updated[:, lo:hi], in0=placed[:, lo:hi], scalar=gain[:], in1=decayed_ps[b][:], op0=ALU.mult, op1=ALU.add
             )
-        result = keep.tile([P, J], F32, name="result")
+        result = keep.tile([P, J], F32, name="result", align_bytes=256)
         for h in range(2):
             lo, hi = h * J // 2, (h + 1) * J // 2
             nc.vector.tensor_copy(result[:, lo:hi].bitcast(U32), updated[:].bitcast(U32).indirect(cands[:, lo // 16 : hi // 16]))

@@ -53,32 +53,32 @@ def tile_attend_evictscores_heads_kernel(tc, query, keys, mass, dec, offs, offs2
             raw = keep.tile([P, 2, 2, width], F32, name=f"late_raw{lo}", align_bytes=256)
             nc.sync.dma_start(out=raw[:], in_=k_view[:, :, :, lo : lo + width])
             late_raw.append(raw)
-        slots = keep.tile([P, I // 16], U16, name="slots")
+        slots = keep.tile([P, I // 16], U16, name="slots", align_bytes=256)
         nc.sync.dma_start(slots[:], offs)
-        dec_raw = keep.tile([P, 1], F32, name="dec_raw")
+        dec_raw = keep.tile([P, 1], F32, name="dec_raw", align_bytes=256)
         nc.sync.dma_start(out=dec_raw[:], in_=dec)
         mass_banks = []
         for lo in range(HEAD, VEC_COLS, BANK):
             part = keep.tile([P, BANK], F32, name=f"mass{lo}", align_bytes=256)
             nc.sync.dma_start(out=part[:], in_=mass[:, lo : lo + BANK])
             mass_banks.append(part)
-        mass_head = keep.tile([P, HEAD], F32, name="mass_head", tag="head_p")
+        mass_head = keep.tile([P, HEAD], F32, name="mass_head", tag="head_p", align_bytes=256)
         nc.sync.dma_start(out=mass_head[:], in_=mass[:, :HEAD])
-        mass_hi = keep.tile([P, T - VEC_COLS], F32, name="mass_hi")
+        mass_hi = keep.tile([P, T - VEC_COLS], F32, name="mass_hi", align_bytes=256)
         nc.sync.dma_start(out=mass_hi[:], in_=mass[:, VEC_COLS:])
-        cands = keep.tile([P, J // 16], U16, name="cands")
+        cands = keep.tile([P, J // 16], U16, name="cands", align_bytes=256)
         nc.sync.dma_start(cands[:], offs2)
 
-        placed = keep.tile([P, T], F32, name="placed")
+        placed = keep.tile([P, T], F32, name="placed", align_bytes=256)
         nc.vector.memset(placed[:], 0.0)
-        ident = keep.tile([P, P], F32, name="ident")
+        ident = keep.tile([P, P], F32, name="ident", align_bytes=256)
         make_identity(nc, ident[:])
 
-        q_bf = keep.tile([P, Q, PACK], BF16, name="q_bf", align_bytes=64)
-        q_codes = keep.tile([P, Q], U32, name="q_codes", align_bytes=64)
-        q_scales = keep.tile([P, Q], U8, name="q_scales", align_bytes=64)
-        k_codes = keep.tile([P, T], U32, name="k_codes", align_bytes=64)
-        k_scales = keep.tile([P, T], U8, name="k_scales", align_bytes=64)
+        q_bf = keep.tile([P, Q, PACK], BF16, name="q_bf", align_bytes=256)
+        q_codes = keep.tile([P, Q], U32, name="q_codes", align_bytes=256)
+        q_scales = keep.tile([P, Q], U8, name="q_scales", align_bytes=256)
+        k_codes = keep.tile([P, T], U32, name="k_codes", align_bytes=256)
+        k_scales = keep.tile([P, T], U8, name="k_scales", align_bytes=256)
         on_vector, on_scalar = nc.vector.tensor_copy, nc.scalar.copy
         staged = {}
 
@@ -91,7 +91,7 @@ def tile_attend_evictscores_heads_kernel(tc, query, keys, mass, dec, offs, offs2
                 c = max(n for n, (t0, width) in enumerate(LATE_LOADS) if t0 <= lo)
                 raw = late_raw[c][:, :, :, lo - LATE_LOADS[c][0] : hi - LATE_LOADS[c][0]]
             if into is None:
-                into = keep.tile([P, hi - lo, PACK], BF16, name=f"staged{lo}", tag=f"staged{lo}", align_bytes=64)[:]
+                into = keep.tile([P, hi - lo, PACK], BF16, name=f"staged{lo}", tag=f"staged{lo}", align_bytes=256)[:]
             staged[lo] = into
             interleave(copy, into, raw)
 
@@ -150,29 +150,29 @@ def tile_attend_evictscores_heads_kernel(tc, query, keys, mass, dec, offs, offs2
         leave(on_vector, product(5, 1920, (64,)), 1920)
         leave(on_scalar, product(6, 1984, (64,)), 1984)
 
-        dec_sb = keep.tile([P, 1], F32, name="dec_sb", tag="staged1984", align_bytes=64)
+        dec_sb = keep.tile([P, 1], F32, name="dec_sb", tag="staged1984", align_bytes=256)
         nc.gpsimd.tensor_scalar(dec_sb[:], dec_raw[:], 2.0, 0.0, ALU.mult, ALU.add)
-        decayed = keep.tile([P, T], F32, name="decayed")
-        updated = keep.tile([P, T], F32, name="updated")
+        decayed = keep.tile([P, T], F32, name="decayed", align_bytes=256)
+        updated = keep.tile([P, T], F32, name="updated", align_bytes=256)
         for b, part in enumerate(mass_banks):
             lo = HEAD + b * BANK
             nc.gpsimd.tensor_scalar(decayed[:, lo : lo + BANK], part[:], dec_sb[:], 0.0, ALU.mult, ALU.add)
         nc.gpsimd.tensor_scalar(decayed[:, VEC_COLS:], mass_hi[:], dec_sb[:], 0.0, ALU.mult, ALU.add)
-        listed = keep.tile([P, I + 1], F32, name="listed", tag="listed_late")
+        listed = keep.tile([P, I + 1], F32, name="listed", tag="listed_late", align_bytes=256)
         nc.scalar.activation(out=listed[:, :I], in_=scores[:].indirect(slots[:]), func=ACT.Copy, scale=-1.0)
-        listed_a = keep.tile([P, I // 2], F32, name="listed_a", tag="listed_a")
+        listed_a = keep.tile([P, I // 2], F32, name="listed_a", tag="listed_a", align_bytes=256)
         nc.vector.tensor_copy(listed_a[:].bitcast(U32), scores[:].bitcast(U32).indirect(slots[:, : I // 32]))
         neg_first = keep.tile([P, 1], F32, name="neg_first")
         nc.vector.tensor_reduce(out=neg_first[:], in_=listed_a[:, :FIRST], axis=mybir.AxisListType.X, op=ALU.max, negate=True)
         nc.vector.tensor_reduce(out=listed[:, I:], in_=listed_a[:, FIRST:], axis=mybir.AxisListType.X, op=ALU.max, negate=True)
-        lowered = keep.tile([P, I // 2 + 1], F32, name="lowered")
+        lowered = keep.tile([P, I // 2 + 1], F32, name="lowered", align_bytes=256)
         neg_shift = keep.tile([P, 1], F32, name="neg_shift")
         nc.vector.tensor_scalar(lowered[:], listed[:, I // 2 :], MARGIN, neg_first[:], ALU.add, ALU.min, accum_out=neg_shift[:])
-        p_first = keep.tile([P, FIRST], F32, name="p_first")
+        p_first = keep.tile([P, FIRST], F32, name="p_first", align_bytes=256)
         nc.scalar.activation(out=p_first[:], in_=listed_a[:, :FIRST], func=ACT.Exp, bias=neg_first[:])
-        decayed_head = keep.tile([P, HEAD], F32, name="decayed_head", tag="listed_a")
+        decayed_head = keep.tile([P, HEAD], F32, name="decayed_head", tag="listed_a", align_bytes=256)
         nc.scalar.activation(out=decayed_head[:], in_=mass_head[:], func=ACT.Copy, scale=dec_sb[:])
-        p_all = keep.tile([P, I], F32, name="p_all", tag="head_p")
+        p_all = keep.tile([P, I], F32, name="p_all", tag="head_p", align_bytes=256)
         p_sum = keep.tile([P, 1], F32, name="p_sum")
         nc.scalar.activation(out=p_all[:], in_=listed[:, :I], func=ACT.Exp, scale=-1.0, bias=neg_shift[:], accum_out=p_sum[:])
         nc.vector.tensor_copy(placed[:].indirect(slots[:, : FIRST // 16]), p_first[:])
@@ -183,7 +183,7 @@ def tile_attend_evictscores_heads_kernel(tc, query, keys, mass, dec, offs, offs2
         gain = keep.tile([P, 1], F32, name="gain")
         nc.vector.tensor_scalar(gain[:], inv_sum[:], 1024.0, None, ALU.mult)
 
-        late = keep.tile([P, VEC_COLS - HEAD], F32, name="late", tag="listed_late")
+        late = keep.tile([P, VEC_COLS - HEAD], F32, name="late", tag="listed_late", align_bytes=256)
         spans = [(lo, min(lo + BANK, VEC_COLS)) for lo in range(HEAD, VEC_COLS, BANK)]
         turned = []
         for b, (lo, hi) in enumerate(spans):
@@ -199,9 +199,9 @@ def tile_attend_evictscores_heads_kernel(tc, query, keys, mass, dec, offs, offs2
                 nc.tensor.transpose(back[:, j - lo : j - lo + P], late[:, j - HEAD : j - HEAD + P], ident[:])
             decayed_ps.append(back)
         split = VEC_COLS + OWN
-        weights_own = keep.tile([P, OWN], F32, name="weights_own")
+        weights_own = keep.tile([P, OWN], F32, name="weights_own", align_bytes=256)
         nc.gpsimd.tensor_scalar(weights_own[:], placed[:, VEC_COLS:split], gain[:], 0.0, ALU.mult, ALU.add)
-        weights_rest = keep.tile([P, T - split], F32, name="weights_rest", tag="listed_late")
+        weights_rest = keep.tile([P, T - split], F32, name="weights_rest", tag="listed_late", align_bytes=256)
         nc.scalar.activation(out=weights_rest[:], in_=placed[:, split:], func=ACT.Copy, scale=gain[:])
         nc.gpsimd.tensor_tensor(updated[:, VEC_COLS:split], weights_own[:], decayed[:, VEC_COLS:split], ALU.add)
         nc.gpsimd.tensor_tensor(updated[:, split:], weights_rest[:], decayed[:, split:], ALU.add)

@@ -42,15 +42,15 @@ def tile_attend_evictscores_heads_kernel(tc, query, keys, mass, dec, offs, offs2
         psum = ctx.enter_context(tc.psum_pool(name="psum", bufs=1))
 
         k_view = keys.rearrange("(p h l) t -> p h l t", h=2, l=2)
-        first_raw = keep.tile([P, 2, 2, HALF], F32, name="first_raw", align_bytes=256)
+        first_raw = keep.tile([P, 2, 2, HALF], F32, name="first_raw", align_bytes=4096)
         nc.sync.dma_start(out=first_raw[:], in_=k_view[:, :, :, :HALF])
-        q_raw = keep.tile([P, 2, 2, Q], F32, name="q_raw", align_bytes=256)
+        q_raw = keep.tile([P, 2, 2, Q], F32, name="q_raw", align_bytes=4096)
         nc.sync.dma_start(out=q_raw[:], in_=query.rearrange("(p h l) q -> p h l q", h=2, l=2))
-        second_raw = keep.tile([P, 2, 2, TAIL - HALF], F32, name="second_raw", tag="scores", align_bytes=256)
+        second_raw = keep.tile([P, 2, 2, TAIL - HALF], F32, name="second_raw", tag="scores", align_bytes=4096)
         nc.sync.dma_start(out=second_raw[:], in_=k_view[:, :, :, HALF:TAIL])
         late_raw = []
         for lo, width in LATE_LOADS:
-            raw = keep.tile([P, 2, 2, width], F32, name=f"late_raw{lo}", align_bytes=256)
+            raw = keep.tile([P, 2, 2, width], F32, name=f"late_raw{lo}", align_bytes=4096)
             nc.sync.dma_start(out=raw[:], in_=k_view[:, :, :, lo : lo + width])
             late_raw.append(raw)
         slots = keep.tile([P, I // 16], U16, name="slots", align_bytes=256)
@@ -59,7 +59,7 @@ def tile_attend_evictscores_heads_kernel(tc, query, keys, mass, dec, offs, offs2
         nc.sync.dma_start(out=dec_raw[:], in_=dec)
         mass_banks = []
         for lo in range(HEAD, VEC_COLS, BANK):
-            part = keep.tile([P, BANK], F32, name=f"mass{lo}", align_bytes=256)
+            part = keep.tile([P, BANK], F32, name=f"mass{lo}", align_bytes=4096)
             nc.sync.dma_start(out=part[:], in_=mass[:, lo : lo + BANK])
             mass_banks.append(part)
         mass_head = keep.tile([P, HEAD], F32, name="mass_head", tag="head_p", align_bytes=256)
@@ -137,7 +137,7 @@ def tile_attend_evictscores_heads_kernel(tc, query, keys, mass, dec, offs, offs2
         quantise(1664, 1792)
         stage(on_vector, 1792, 1920)
         quantise(1792, 1920)
-        scores = keep.tile([P, T], F32, name="scores", tag="scores", align_bytes=256)
+        scores = keep.tile([P, T], F32, name="scores", tag="scores", align_bytes=4096)
         stage(on_vector, 1920, 1984, scores[:, 1536:1664].bitcast(BF16).rearrange("p (w j) -> p w j", j=PACK))
         stage(on_scalar, 1984, 2048)
         quantise(1920, 1984)
@@ -212,7 +212,7 @@ def tile_attend_evictscores_heads_kernel(tc, query, keys, mass, dec, offs, offs2
             nc.vector.scalar_tensor_tensor(
                 out=updated[:, lo:hi], in0=placed[:, lo:hi], scalar=gain[:], in1=decayed_ps[b][:], op0=ALU.mult, op1=ALU.add
             )
-        result = keep.tile([P, J], F32, name="result", align_bytes=256)
+        result = keep.tile([P, J], F32, name="result", align_bytes=4096)
         for h in range(2):
             lo, hi = h * J // 2, (h + 1) * J // 2
             nc.vector.tensor_copy(result[:, lo:hi].bitcast(U32), updated[:].bitcast(U32).indirect(cands[:, lo // 16 : hi // 16]))

@@ -19,7 +19,7 @@ P = 128
 PACK = 4
 HALF = T // 2
 TAIL = 1536
-LATE_LOADS = ((1536, 256), (1792, 128), (1920, 128))
+LATE_LOADS = ((1536, 256), (1792, 192), (1984, 64))
 BANK = 512
 FIRST = 160
 MARGIN = 80.0
@@ -138,8 +138,8 @@ def tile_attend_evictscores_heads_kernel(tc, query, keys, mass, dec, offs, offs2
         stage(on_vector, 1792, 1920)
         quantise(1792, 1920)
         scores = keep.tile([P, T], F32, name="scores", tag="scores", align_bytes=4096)
-        stage(on_vector, 1920, 1984, scores[:, 1536:1664].bitcast(BF16).rearrange("p (w j) -> p w j", j=PACK))
-        stage(on_scalar, 1984, 2048)
+        stage(on_scalar, 1920, 1984, scores[:, 1536:1664].bitcast(BF16).rearrange("p (w j) -> p w j", j=PACK))
+        stage(on_vector, 1984, 2048)
         quantise(1920, 1984)
         quantise(1984, 2048)
         leave(on_scalar, product(0, 0, (512,)), 0)

from contextlib import ExitStack

import concourse.mybir as mybir
from concourse.masks import make_identity

D, T, Q, I, J = 512, 2048, 128, 512, 512
FLOPS = 2 * D * T * Q

F32 = mybir.dt.float32
BF16 = mybir.dt.bfloat16
U32 = mybir.dt.uint32
U16 = mybir.dt.uint16
U8 = mybir.dt.uint8
FP8X4 = mybir.dt.float8_e4m3fn_x4
ALU = mybir.AluOpType
ACT = mybir.ActivationFunctionType

P = 128
PACK = 4
HALF = T // 2
TAIL = 1536
LATE_LOADS = ((1536, 256), (1792, 192), (1984, 64))
BANK = 512
FIRST = 160
MARGIN = 80.0
HEAD = 64
VEC_COLS = 1600
OWN = 128


def interleave(copy, grouped, raw):
    copy(
        out=grouped.rearrange("p (c i) (h l) -> p c h l i", i=2, l=2),
        in_=raw.rearrange("p h l (c i) -> p c h l i", i=2),
    )


def tile_attend_evictscores_heads_kernel(tc, query, keys, mass, dec, offs, offs2, out):
    nc = tc.nc
    with ExitStack() as ctx:
        keep = ctx.enter_context(tc.tile_pool(name="keep", bufs=1))
        psum = ctx.enter_context(tc.psum_pool(name="psum", bufs=1))

        k_view = keys.rearrange("(p h l) t -> p h l t", h=2, l=2)
        first_raw = keep.tile([P, 2, 2, HALF], F32, name="first_raw", align_bytes=4096)
        nc.sync.dma_start(out=first_raw[:], in_=k_view[:, :, :, :HALF])
        q_raw = keep.tile([P, 2, 2, Q], F32, name="q_raw", align_bytes=4096)
        nc.sync.dma_start(out=q_raw[:], in_=query.rearrange("(p h l) q -> p h l q", h=2, l=2))
        second_raw = keep.tile([P, 2, 2, TAIL - HALF], F32, name="second_raw", tag="scores", align_bytes=4096)
        nc.sync.dma_start(out=second_raw[:], in_=k_view[:, :, :, HALF:TAIL])
        late_raw = []
        for lo, width in LATE_LOADS:
            raw = keep.tile([P, 2, 2, width], F32, name=f"late_raw{lo}", align_bytes=4096)
            nc.sync.dma_start(out=raw[:], in_=k_view[:, :, :, lo : lo + width])
            late_raw.append(raw)
        slots = keep.tile([P, I // 16], U16, name="slots", align_bytes=256)
        nc.sync.dma_start(slots[:], offs)
        dec_raw = keep.tile([P, 1], F32, name="dec_raw", align_bytes=256)
        nc.sync.dma_start(out=dec_raw[:], in_=dec)
        mass_banks = []
        for lo in range(HEAD, VEC_COLS, BANK):
            part = keep.tile([P, BANK], F32, name=f"mass{lo}", align_bytes=4096)
            nc.sync.dma_start(out=part[:], in_=mass[:, lo : lo + BANK])
            mass_banks.append(part)
        mass_head = keep.tile([P, HEAD], F32, name="mass_head", tag="head_p", align_bytes=256)
        nc.sync.dma_start(out=mass_head[:], in_=mass[:, :HEAD])
        mass_hi = keep.tile([P, T - VEC_COLS], F32, name="mass_hi", align_bytes=256)
        nc.sync.dma_start(out=mass_hi[:], in_=mass[:, VEC_COLS:])
        cands = keep.tile([P, J // 16], U16, name="cands", align_bytes=256)
        nc.sync.dma_start(cands[:], offs2)

        placed = keep.tile([P, T], F32, name="placed", align_bytes=256)
        nc.vector.memset(placed[:], 0.0)
        ident = keep.tile([P, P], F32, name="ident", align_bytes=256)
        make_identity(nc, ident[:])

        q_bf = keep.tile([P, Q, PACK], BF16, name="q_bf", align_bytes=256)
        q_codes = keep.tile([P, Q], U32, name="q_codes", align_bytes=256)
        q_scales = keep.tile([P, Q], U8, name="q_scales", align_bytes=256)
        k_codes = keep.tile([P, T], U32, name="k_codes", align_bytes=256)
        k_scales = keep.tile([P, T], U8, name="k_scales", align_bytes=256)
        on_vector, on_scalar = nc.vector.tensor_copy, nc.scalar.copy
        staged = {}

        def stage(copy, lo, hi, into=None):
            if lo < HALF:
                raw = first_raw[:, :, :, lo:hi]
            elif lo < TAIL:
                raw = second_raw[:, :, :, lo - HALF : hi - HALF]
            else:
                c = max(n for n, (t0, width) in enumerate(LATE_LOADS) if t0 <= lo)
                raw = late_raw[c][:, :, :, lo - LATE_LOADS[c][0] : hi - LATE_LOADS[c][0]]
            if into is None:
                into = keep.tile([P, hi - lo, PACK], BF16, name=f"staged{lo}", tag=f"staged{lo}", align_bytes=256)[:]
            staged[lo] = into
            interleave(copy, into, raw)

        def quantise(lo, hi):
            nc.vector.quantize_mx(
                out=k_codes[:, lo:hi].bitcast(FP8X4), scales=k_scales[:, lo:hi], in_=staged[lo].rearrange("p w j -> p (w j)")
            )

        def product(bank, lo, groups):
            acc = psum.tile([Q, sum(groups)], F32, name=f"acc{lo}", tag=f"bank{bank}")
            at = 0
            for n in groups:
                nc.tensor.matmul_mx(
                    out=acc[:, at : at + n],
                    lhsT=q_codes[:].bitcast(FP8X4),
                    lhsT_scale=q_scales[:],
                    rhs=k_codes[:, lo + at : lo + at + n].bitcast(FP8X4),
                    rhs_scale=k_scales[:, lo + at : lo + at + n],
                    start=True,
                    stop=True,
                )
                at += n
            return acc

        def leave(copy, acc, lo):
            copy(out=scores[:, lo : lo + acc.shape[1]], in_=acc[:])

        stage(on_vector, 0, 512)
        interleave(on_vector, q_bf[:], q_raw[:])
        stage(on_scalar, 512, 768)
        stage(on_scalar, 768, 1024)
        quantise(0, 512)
        nc.vector.quantize_mx(out=q_codes[:].bitcast(FP8X4), scales=q_scales[:], in_=q_bf[:].rearrange("p w j -> p (w j)"))
        quantise(512, 768)
        quantise(768, 1024)
        stage(on_vector, 1024, 1280)
        stage(on_scalar, 1280, 1536)
        quantise(1024, 1280)
        quantise(1280, 1536)
        stage(on_vector, 1536, 1664)
        stage(on_vector, 1664, 1792)
        quantise(1536, 1664)
        quantise(1664, 1792)
        stage(on_vector, 1792, 1920)
        quantise(1792, 1920)
        scores = keep.tile([P, T], F32, name="scores", tag="scores", align_bytes=4096)
        stage(on_scalar, 1920, 1984, scores[:, 1536:1664].bitcast(BF16).rearrange("p (w j) -> p w j", j=PACK))
        stage(on_vector, 1984, 2048)
        quantise(1920, 1984)
        quantise(1984, 2048)
        leave(on_scalar, product(0, 0, (512,)), 0)
        leave(on_scalar, product(1, 512, (256, 256)), 512)
        leave(on_scalar, product(2, 1024, (256, 256)), 1024)
        leave(on_vector, product(3, 1536, (256,)), 1536)
        leave(on_scalar, product(4, 1792, (128,)), 1792)
        leave(on_vector, product(5, 1920, (64,)), 1920)
        leave(on_scalar, product(6, 1984, (64,)), 1984)

        dec_sb = keep.tile([P, 1], F32, name="dec_sb", tag="staged1984", align_bytes=256)
        nc.gpsimd.tensor_scalar(dec_sb[:], dec_raw[:], 2.0, 0.0, ALU.mult, ALU.add)
        decayed = keep.tile([P, T], F32, name="decayed", align_bytes=256)
        updated = keep.tile([P, T], F32, name="updated", align_bytes=256)
        for b, part in enumerate(mass_banks):
            lo = HEAD + b * BANK
            nc.gpsimd.tensor_scalar(decayed[:, lo : lo + BANK], part[:], dec_sb[:], 0.0, ALU.mult, ALU.add)
        nc.gpsimd.tensor_scalar(decayed[:, VEC_COLS:], mass_hi[:], dec_sb[:], 0.0, ALU.mult, ALU.add)
        listed = keep.tile([P, I + 1], F32, name="listed", tag="listed_late", align_bytes=256)
        nc.scalar.activation(out=listed[:, :I], in_=scores[:].indirect(slots[:]), func=ACT.Copy, scale=-1.0)
        listed_a = keep.tile([P, I // 2], F32, name="listed_a", tag="listed_a", align_bytes=256)
        nc.vector.tensor_copy(listed_a[:].bitcast(U32), scores[:].bitcast(U32).indirect(slots[:, : I // 32]))
        neg_first = keep.tile([P, 1], F32, name="neg_first")
        nc.vector.tensor_reduce(out=neg_first[:], in_=listed_a[:, :FIRST], axis=mybir.AxisListType.X, op=ALU.max, negate=True)
        nc.vector.tensor_reduce(out=listed[:, I:], in_=listed_a[:, FIRST:], axis=mybir.AxisListType.X, op=ALU.max, negate=True)
        lowered = keep.tile([P, I // 2 + 1], F32, name="lowered", align_bytes=256)
        neg_shift = keep.tile([P, 1], F32, name="neg_shift")
        nc.vector.tensor_scalar(lowered[:], listed[:, I // 2 :], MARGIN, neg_first[:], ALU.add, ALU.min, accum_out=neg_shift[:])
        p_first = keep.tile([P, FIRST], F32, name="p_first", align_bytes=256)
        nc.scalar.activation(out=p_first[:], in_=listed_a[:, :FIRST], func=ACT.Exp, bias=neg_first[:])
        decayed_head = keep.tile([P, HEAD], F32, name="decayed_head", tag="listed_a", align_bytes=256)
        nc.scalar.activation(out=decayed_head[:], in_=mass_head[:], func=ACT.Copy, scale=dec_sb[:])
        p_all = keep.tile([P, I], F32, name="p_all", tag="head_p", align_bytes=256)
        p_sum = keep.tile([P, 1], F32, name="p_sum")
        nc.scalar.activation(out=p_all[:], in_=listed[:, :I], func=ACT.Exp, scale=-1.0, bias=neg_shift[:], accum_out=p_sum[:])
        nc.vector.tensor_copy(placed[:].indirect(slots[:, : FIRST // 16]), p_first[:])
        inv_sum = keep.tile([P, 1], F32, name="inv_sum")
        nc.vector.reciprocal(out=inv_sum[:], in_=p_sum[:])
        nc.vector.tensor_copy(placed[:].indirect(slots[:, FIRST // 16 :]), p_all[:, FIRST:])

        gain = keep.tile([P, 1], F32, name="gain")
        nc.vector.tensor_scalar(gain[:], inv_sum[:], 1024.0, None, ALU.mult)

        late = keep.tile([P, VEC_COLS - HEAD], F32, name="late", tag="listed_late", align_bytes=256)
        spans = [(lo, min(lo + BANK, VEC_COLS)) for lo in range(HEAD, VEC_COLS, BANK)]
        turned = []
        for b, (lo, hi) in enumerate(spans):
            turn = psum.tile([P, hi - lo], F32, name=f"turn{b}", tag=f"bank{(7 + b) % 8}")
            for j in range(lo, hi, P):
                nc.tensor.transpose(turn[:, j - lo : j - lo + P], decayed[:, j : j + P], ident[:])
            turned.append(turn)
        decayed_ps = []
        for b, (lo, hi) in enumerate(spans):
            nc.scalar.copy(out=late[:, lo - HEAD : hi - HEAD], in_=turned[b][:])
            back = psum.tile([P, hi - lo], F32, name=f"back{b}", tag=f"bank{3 + b}")
            for j in range(lo, hi, P):
                nc.tensor.transpose(back[:, j - lo : j - lo + P], late[:, j - HEAD : j - HEAD + P], ident[:])
            decayed_ps.append(back)
        split = VEC_COLS + OWN
        weights_own = keep.tile([P, OWN], F32, name="weights_own", align_bytes=256)
        nc.gpsimd.tensor_scalar(weights_own[:], placed[:, VEC_COLS:split], gain[:], 0.0, ALU.mult, ALU.add)
        weights_rest = keep.tile([P, T - split], F32, name="weights_rest", tag="listed_late", align_bytes=256)
        nc.scalar.activation(out=weights_rest[:], in_=placed[:, split:], func=ACT.Copy, scale=gain[:])
        nc.gpsimd.tensor_tensor(updated[:, VEC_COLS:split], weights_own[:], decayed[:, VEC_COLS:split], ALU.add)
        nc.gpsimd.tensor_tensor(updated[:, split:], weights_rest[:], decayed[:, split:], ALU.add)
        nc.vector.scalar_tensor_tensor(
            out=updated[:, :HEAD], in0=placed[:, :HEAD], scalar=gain[:], in1=decayed_head[:], op0=ALU.mult, op1=ALU.add
        )
        for b, (lo, hi) in enumerate(spans):
            nc.vector.scalar_tensor_tensor(
                out=updated[:, lo:hi], in0=placed[:, lo:hi], scalar=gain[:], in1=decayed_ps[b][:], op0=ALU.mult, op1=ALU.add
            )
        result = keep.tile([P, J], F32, name="result", align_bytes=4096)
        for h in range(2):
            lo, hi = h * J // 2, (h + 1) * J // 2
            nc.vector.tensor_copy(result[:, lo:hi].bitcast(U32), updated[:].bitcast(U32).indirect(cands[:, lo // 16 : hi // 16]))
            nc.sync.dma_start(out=out[:, lo:hi], in_=result[:, lo:hi])
